import numpy as np, ml_dtypes
CORES = [3,7,11,15,131,135,139,143]
N = 8
import mx_ref
BF = ml_dtypes.bfloat16
def gentries(a):
    return np.ascontiguousarray(a.reshape(8, 16, -1).transpose(0, 2, 1)).reshape(8, -1)
def gtable(e):
    e = np.asarray(e); return np.ascontiguousarray(e.reshape(8, -1, 16).transpose(0, 2, 1)).reshape(128, -1).astype(np.int32)
def gcols(t, e):
    v = np.concatenate([t.reshape(8, 16, -1, 4), np.zeros((8, 16, 1, 4), BF)], axis=2)
    return np.ascontiguousarray(np.stack([v[g][:, e[g]] for g in range(8)])).reshape(128, -1)
def tile(rs):
    return np.stack(rs, axis=2).reshape(128, -1).astype(BF)
def pick(q, e):
    c = np.concatenate([q[0].reshape(128, -1, 4), np.zeros((128, 1, 4), np.uint8)], axis=1); s = np.concatenate([q[1], np.ones((16, 1), np.uint8)], axis=1)
    return (np.ascontiguousarray(c[:, e].reshape(128, -1)), np.ascontiguousarray(s[:, e]))
def join(*qs):
    return (np.concatenate([q[0] for q in qs], axis=1), np.concatenate([q[1] for q in qs], axis=1))
def put(q, e, v):
    c, s = q[0].reshape(128, -1, 4).copy(), q[1].copy(); c[:, e] = v[0].reshape(128, -1, 4); s[:, e] = v[1]
    return (c.reshape(128, -1), s)
def pk(c, s):
    return (np.ascontiguousarray(c), mx_ref.live(s))
def emit(q):
    return q[0], q[1]
def packed(v, rng):
    q = [mx_ref.quantize(np.ascontiguousarray(v[r])) for r in range(N)]
    return np.stack([a for a, b in q]), np.stack([mx_ref.plane(b, rng) for a, b in q])
def values_of_codes():
    e, c = np.zeros((128, 128, 4), np.float32), np.zeros((128, 2, 4), np.uint8)
    e[np.arange(128), np.arange(128), 0] = 1
    c[:127, :, 0] = np.arange(256).reshape(2, 128).T[:127]
    return mx_ref.matmul(mx_ref.quantize(e.reshape(128, 512).astype(BF)), (c.reshape(128, 8), np.full((16, 2), 127, np.uint8))).T.reshape(-1).astype(np.float64)
CODE_VALUE, SCALE_VALUE = values_of_codes(), 2.0 ** (np.arange(256) - 127.0)
def decode(q):
    return (CODE_VALUE[q[0]].reshape(16, 8, -1, 4) * SCALE_VALUE[q[1]][:, None, :, None] + 0.0).reshape(128, -1).astype(np.float32)
def f(rng, *shape):
    return mx_ref.flush((rng.standard_normal(shape, dtype=np.float32) * np.exp2(rng.integers(-2, 3, shape[:-1] + (1,)))).astype(BF))
def wide(rng, *shape, cols=0):
    v = rng.standard_normal(shape, dtype=np.float32) * np.exp2(rng.integers(-12, 13, shape)).astype(np.float32)
    if cols: v *= np.repeat(np.exp2(rng.integers(-cols, cols + 1, shape[:-2] + (1, shape[-1] // 4))) * (rng.random(shape[:-2] + (1, shape[-1] // 4)) > 0.0625), 4, axis=-1).astype(np.float32)
    return mx_ref.flush(v.astype(BF))
C, T, R = 320, 160, 3
STEP = [1, 2, 4]
def big(v):
    v = v.astype(np.float32)
    v[np.abs(v) < np.float32(2.0 ** -16)] = 0
    return v.astype(BF)
def numbers_of(rng):
    return {"x": big(f(rng, N, 128, 4 * C)), "bm": big(f(rng, N, 128, 4 * C)), "u": np.array(f(rng, N, 128, 512)), "v": np.array(f(rng, N, 128, 512))}
def stored(a):
    return {"co": np.stack([gtable(e) for e in a]), "cn": np.stack([gtable(np.concatenate([a[(r + s) % N][:, :T] for s in STEP], axis=1)) for r in range(N)])}
def anywhere(rng):
    return rng.integers(0, C, (N, 8, C))
def weights(rng, w):
    c, p = packed(w, rng)
    return {"wc": c, "ws": p}
def straight(rng, size):
    w = np.zeros((N, 128, 4, 128, 4), np.float32)
    i = np.arange(128)
    for k in range(4): w[:, i, k, i, k] = np.tile(size, 8)
    return weights(rng, w.reshape(N, 128, 2048).astype(BF))
def signs(rng):
    return np.stack([rng.permutation(8) % 2 * 2.0 - 1.0 for r in range(N)])
def setup_inputs(rng):
    return {**numbers_of(rng), **stored(anywhere(rng)), **weights(rng, f(rng, N, 128, 2048))}
def setup_inputs_ties(rng):
    d = numbers_of(rng)
    e = rng.permutation(N)
    x = d["x"].reshape(N, 8, 16, C, 4)
    bm = d["bm"].reshape(N, 8, 16, C, 4)
    for r in range(N):
        k = np.zeros(C, int) if r == e[0] else rng.permutation(C) % 3
        a = x[r][:, :8, :3].copy()
        a[:, :, 2] = 0
        x[r][:, :8] = a[:, :, k]
        bm[r][:, :8] = bm[r][:, :8, :1].copy()
        bm[r][rng.permutation(8) < 3, :8] = 0
    x[e[1]] = 0
    u = d["u"].reshape(N, 8, 16, 128, 4)
    u[:, :, 8:, ::16] = 0
    for g in range(8):
        for h in range(8):
            if h != g: u[:, h, :, 16 * g] = 0
    w = np.array(f(rng, N, 128, 2048)).reshape(N, 8, 16, 4, 8, 16, 4)
    w[:, :, :, :, :, :8] = 0
    return {"x": x.reshape(N, 128, 4 * C), "bm": bm.reshape(N, 128, 4 * C), "u": u.reshape(N, 128, 512), "v": d["v"], **stored(anywhere(rng)), **weights(rng, w.reshape(N, 128, 2048))}
def setup_inputs_near(rng):
    d = numbers_of(rng)
    o = rng.permutation(N)
    x = d["x"].astype(np.float32).reshape(N, 8, 16, C, 4)
    bm = d["bm"].astype(np.float32).reshape(N, 8, 16, C, 4)
    u = d["u"].astype(np.float32).reshape(N, 128, 128, 4)
    u[:, :, ::16] = 0
    for z in (x, bm):
        z[:, :, 11:] = rng.integers(4, 8, (N, 8, 5, C, 4)) * rng.choice([-1.0, 1.0], (N, 8, 5, C, 4)) * 2.0 ** -20
        for i in (0, 8, 9, 10): z[:, :, i] = 0
    sg = signs(rng)
    for r in range(N):
        small = o[r] % 2 == 1
        e = 2.0 ** -30 if small else 2.0 ** -23
        k = 1.0 if o[r] % 4 == 0 else 2.0 ** -30
        s = np.arange(C) // 2 if o[r] // 2 % 2 == 0 else np.arange(C) % (C // 2) // 2
        digit = (s[:, None] >> np.arange(8)) & 1
        turn = rng.choice([-1.0, 1.0])
        for g in range(8):
            a = (digit - 1 if small and sg[r, g] < 0 else digit) * e * np.exp2(np.arange(8))
            x[r, g, 8] = a[:, :4]
            x[r, g, 9] = a[:, 4:]
            if not small: x[r, g, 0, :, 0] = sg[r, g]
            if g % 2:
                j = int(rng.integers(C // 4))
                x[r, g, 0, j, 0] = -2.0 ** 30
                x[r, g, 0, j + C // 2, 0] = -2.0 ** 30
            one = rng.choice([-1.0, 1.0])
            bm[r, g, 10, 0, 0] = one * (8 if small and g < 4 else 512) * e
            h = 16 * g
            u[r, h, h, 0] = k
            u[r, h + 8:h + 10, h] = k
            u[r, h + 10, h, 0] = one * (turn if g % 2 else -turn) * k
            if small and g < 2:
                bm[r, g, 10, 0, 1] = bm[r, g, 10, 0, 0]
                u[r, h + 10, h, 1] = -u[r, h + 10, h, 0]
                u[r, h + 10, h, 0] *= 1.125
    size = np.full(16, 32.0)
    size[[0, 8, 9, 10]] = 0
    return {"x": x.reshape(N, 128, 4 * C).astype(BF), "bm": bm.reshape(N, 128, 4 * C).astype(BF), "u": u.reshape(N, 128, 512).astype(BF), "v": d["v"], **stored(anywhere(rng)), **straight(rng, size)}
def setup_inputs_huge(rng):
    d = numbers_of(rng)
    o = rng.permutation(N)
    x = 2.0 ** 30 * (0.5 + 0.1 * rng.random((N, 128, C, 4)))
    c = np.stack([rng.permutation(C) % 2 * 2.0 - 1.0 for r in range(N)])
    c[o < N // 2] = 1
    x *= c[:, None, :, None]
    bm = 2.0 ** 27 * (0.5 + 0.5 * rng.random((N, 128, 4 * C))) * (o % 2 * 2.0 - 1.0)[:, None, None]
    u = d["u"].reshape(N, 128, 128, 4)
    a = 2.0 ** 30 * (1 - 0.25 * rng.random((N, 128, 8, 4))) * signs(rng)[:, None, :, None]
    u[:, :, ::16] = a.astype(np.float32).astype(BF)
    return {"x": x.astype(np.float32).reshape(N, 128, 4 * C).astype(BF), "bm": bm.astype(np.float32).astype(BF), "u": u.reshape(N, 128, 512), "v": d["v"], **stored(anywhere(rng)), **straight(rng, np.full(16, 4.0))}
def setup_inputs_coords(rng):
    a = anywhere(rng)
    i = np.arange(C)
    for r in range(N):
        g = rng.permutation(8)
        a[r, g[0]] = int(rng.integers(C))
        a[r, g[1]] = rng.permutation(C) % 2 * (C - 1)
        a[r, g[2]] = i
        a[r, g[3]] = C - 1 - i
        a[r, g[4]] = i % 2
    return {**numbers_of(rng), **stored(a), **weights(rng, f(rng, N, 128, 2048))}
def setup_inputs_spread(rng):
    d = setup_inputs(rng)
    d["x"] = big(wide(rng, N, 128, 4 * C, cols=6))
    d["bm"] = big(wide(rng, N, 128, 4 * C, cols=6))
    return d
def check_inputs(d):
    b = []
    for k in ("x", "bm", "u", "v"):
        a = np.abs(d[k].astype(np.float32))
        if not (np.isfinite(a).all() and ((a == 0) | (a >= 2.0 ** -30) & (a <= 2.0 ** 30)).all()): b.append("a value of " + k)
    for k in ("co", "cn"):
        if ((d[k] < 0) | (d[k] >= C)).any(): b.append("an entry of " + k)
    for r in range(N):
        e = np.concatenate([gentries(d["co"][(r + s) % N])[:, :T] for s in STEP], axis=1)
        if (gentries(d["cn"][r]) != e).any(): b.append("cn isn't what co of other ranks says")
    if (d["wc"] % 128 == 127).any(): b.append("a code of wc that is no number")
    for p in d["ws"]:
        s = mx_ref.live(p)
        if ((s < 1) | (s > 157)).any(): b.append("a scale of ws")
    return b
def reference(x, bm, u, v, co, cn, wc, ws):
    qu = [mx_ref.quantize(u[r]) for r in range(N)]
    lay = [pk(wc[r], ws[r]) for r in range(N)]
    now, beam = [x[r] for r in range(N)], [bm[r] for r in range(N)]
    half = C // 2
    ol = np.zeros((N, 8, 2 * R), np.float32)
    for t in range(R):
        left, sent = [], []
        for r in range(N):
            p = mx_ref.matmul(qu[r], mx_ref.quantize(now[r]))[::16] + np.float32(0.0)
            s = mx_ref.matmul(qu[r], mx_ref.quantize(np.ascontiguousarray(beam[r][:, :16])))[::16, 0]
            k = np.argmax(p.reshape(8, 2, half), axis=2) + np.array([0, half])
            best = np.take_along_axis(p, k, axis=1)
            h = np.where(best[:, 1] > best[:, 0], k[:, 1], k[:, 0])
            c = np.repeat(np.where(s > 0, np.float32(0.5), np.float32(-0.5)), 16)[:, None]
            own = gentries(co[r])
            far = gentries(cn[r])[:, T * t:T * t + T]
            e = np.abs(own - np.repeat(np.take_along_axis(own, k, axis=1), half, axis=1))
            left.append(now[r].astype(np.float32) - c * gcols(beam[r], e).astype(np.float32))
            e = np.abs(far - np.take_along_axis(own, h[:, None], axis=1))
            sent.append(mx_ref.quantize((c * gcols(beam[r], e).astype(np.float32)).astype(BF)))
            ol[r, :, 2 * t:2 * t + 2] = k
        for r in range(N):
            left[r][:, :4 * T] = left[r][:, :4 * T] - decode(sent[(r - STEP[t]) % N])
            now[r] = left[r].astype(BF)
            if t < R - 1:
                q = mx_ref.quantize(now[r])
                beam[r] = tile([mx_ref.matmul(pick(lay[r], np.arange(128 * b, 128 * b + 128)), q) * np.float32(0.015625) + beam[r][:, b::4].astype(np.float32) * np.float32(0.5) for b in range(4)])
    y = np.zeros((N, 128, C), np.float32)
    oc, osc = np.zeros((N, 128, 4 * C), np.uint8), np.zeros((N, 16, C), np.uint8)
    for r in range(N):
        q = mx_ref.quantize(now[r])
        y[r] = mx_ref.matmul(mx_ref.quantize(v[r]), q)
        oc[r], osc[r] = emit(q)
    return {"y": y, "ol": ol, "oc": oc, "osc": osc}

@@ -1,0 +1,502 @@
+from concourse.mybir import dt, AluOpType, ActivationFunctionType
+
+C, H, R = 320, 160, 3
+STEP = [1, 2, 4]
+LOW = -1.0e29
+BF, F32, I32, U16, U8, MX = "bfloat16", "float32", "int32", "uint16", "uint8", "float8_e4m3fn_x4"
+
+SCRATCH = {
+    "pd": ("psum", [128, 2048], F32), "pr": ("psum", [128, 2048], F32),
+    "ut": ("sbuf", [128, 512], BF), "qu": ("sbuf", [128, 128], MX), "su": ("sbuf", [128, 128], U8),
+    "qup": ("sbuf", [128, 128], MX), "sup": ("sbuf", [128, 128], U8),
+    "uli": ("sbuf", [128, 8], I32), "ul16": ("sbuf", [128, 8], U16),
+    "vt": ("sbuf", [128, 512], BF), "qv": ("sbuf", [128, 128], MX), "sv": ("sbuf", [128, 128], U8),
+    "wq": ("sbuf", [128, 512], MX), "wp": ("sbuf", [128, 512], U8),
+    "ones": ("sbuf", [128, 128], BF), "idn": ("sbuf", [128, 128], BF), "em": ("sbuf", [128, 528], BF),
+    "qe": ("sbuf", [128, 512], MX), "se": ("sbuf", [128, 512], U8),
+    "bt": ("sbuf", [128, 4 * C], BF),
+    "sg": ("sbuf", [128, 512], BF),
+    "coi": ("sbuf", [128, 20], I32), "cof": ("sbuf", [128, 20], F32), "co16": ("sbuf", [128, 20], U16),
+    "cni": ("sbuf", [128, 30], I32), "cnf": ("sbuf", [128, 30], F32),
+    "ramp": ("sbuf", [128, C], F32), "tab": ("sbuf", [128, 336], F32),
+    "dm": ("sbuf", [128, 168], F32),
+    "olb": ("sbuf", [128, 8], F32), "olf": ("sbuf", [128, 8], F32),
+    "ysb": ("sbuf", [128, C], F32),
+    "junk": ("sbuf", [128, 9 * H], BF),
+}
+for _t in range(R + 1):
+    SCRATCH["xt%d" % _t] = ("sbuf", [128, 4 * C], BF)
+    SCRATCH["qx%d" % _t] = ("sbuf", [128, C], MX)
+    SCRATCH["sx%d" % _t] = ("sbuf", [128, C], U8)
+for _t in range(R):
+    if _t > 0:
+        SCRATCH["z%d" % _t] = ("sbuf", [128, 4 * C], BF)
+    if _t < R - 1:
+        SCRATCH["zh%d" % _t] = ("sbuf", [128, 4 * C], BF)
+    SCRATCH["cb%d" % _t] = ("sbuf", [128, 4 * C], BF)
+    SCRATCH["e%d" % _t] = ("sbuf", [128, 4 * H], F32)
+    SCRATCH["gt%d" % _t] = ("sbuf", [128, 4 * H], BF)
+    SCRATCH["gq%d" % _t] = ("sbuf", [128, H], MX)
+    SCRATCH["gs%d" % _t] = ("sbuf", [128, H], U8)
+    SCRATCH["lq%d" % _t] = ("sbuf", [128, H], MX)
+    SCRATCH["ls%d" % _t] = ("sbuf", [128, H], U8)
+    SCRATCH["qs%d" % _t] = ("sbuf", [128, 128], MX)
+    SCRATCH["ss%d" % _t] = ("sbuf", [128, 128], U8)
+    SCRATCH["run%d" % _t] = ("sbuf", [128, 336], F32)
+    SCRATCH["sm%d" % _t] = ("sbuf", [128, 96], F32)
+    SCRATCH["of%d" % _t] = ("sbuf", [128, 80], U16)
+
+NPOOL = 140
+SEMAPHORES = ["sent", "arr0", "arr1", "arr2"] + ["s%d" % _i for _i in range(NPOOL)]
+
+ALU, ACT = AluOpType, ActivationFunctionType
+SC, SCS, SCN, SD, SK0, SE1, SH, SE0, SAH, SA0 = 0, 1, 2, 16, 26, 32, 42, 48, 64, 80
+OG, OK0, OE1, OH, OE0, OK1, OG4 = 0, 10, 12, 22, 24, 34, 36
+ORDER = {"chain": "Zsh01clqkf2go3", "window": "abclhdq0s1k2n3gwxy", "last": "al0b1c2d3q"}
+
+
+def build(g, core, T, topo, rank):
+    ops = []
+    Q = {"g": g, "v": g.vector, "s": g.scalar, "t": g.tensor, "y": g.sync}
+
+    def view(name, a, b, step=1):
+        m = 0
+        for c in range(a, b, step):
+            m |= 1 << (c // 512 if name in ("pd", "pr") else c)
+        ap = T[name][:, a:b] if step == 1 else T[name][:, a:b:step]
+        return (ap, [(name, m)])
+
+    def pickv(win, off):
+        return (win[0].indirect(off[0]), win[1] + off[1])
+
+    def op(q, kind, fn, reads, writes):
+        rd, wr = [], []
+        for x in reads:
+            if isinstance(x, tuple):
+                rd += x[1]
+        for x in writes:
+            wr += x[1]
+        ops.append({"q": q, "kind": kind, "fn": fn, "rd": rd, "wr": wr, "set": None})
+
+    def bundle(name):
+        ops[-1]["set"] = name
+
+    def A(x):
+        return x[0] if isinstance(x, tuple) else x
+
+    def dma(q, out, src, after=None):
+        op(q, "dma", lambda: Q[q].dma_start(A(out), A(src)), [src, after], [out] if isinstance(out, tuple) else [])
+
+    def bits(x):
+        return (x[0].bitcast(dt.uint8), x[1])
+
+    def copy(out, src):
+        op("v", "c", lambda: g.vector.tensor_copy(out[0], src[0]), [src], [out])
+
+    def fill(out, val):
+        op("v", "c", lambda: g.vector.memset(out[0], val), [], [out])
+
+    def tt(out, a, b, o):
+        op("v", "c", lambda: g.vector.tensor_tensor(out[0], a[0], b[0], o), [a, b], [out])
+
+    def ts(out, a, s1, s2, o0, o1=None):
+        if o1 is None:
+            op("v", "c", lambda: g.vector.tensor_scalar(out[0], a[0], A(s1), None, o0), [a, s1], [out])
+        else:
+            op("v", "c", lambda: g.vector.tensor_scalar(out[0], a[0], A(s1), A(s2), o0, o1), [a, s1, s2], [out])
+
+    def scan(out, d0, d1):
+        op("v", "c", lambda: g.vector.tensor_tensor_scan(out[0], d0[0], d1[0], LOW, ALU.max, ALU.max), [d0, d1], [out])
+
+    def act(out, src, func, scale=None, bias=None, acc=None):
+        kw = {}
+        if scale is not None:
+            kw["scale"] = A(scale)
+        if bias is not None:
+            kw["bias"] = A(bias)
+        if acc is not None:
+            kw["accum_out"] = acc[0]
+        op("s", "c", lambda: g.scalar.activation(out[0], src[0], func, **kw), [src, scale, bias],
+           [out] + ([acc] if acc is not None else []))
+
+    def quant(q, s, a, b, tile, t0):
+        oq, os_, src = view(q, a, b), view(s, a, b), view(tile, t0, t0 + 4 * (b - a))
+        op("v", "c", lambda: g.vector.quantize_mx(oq[0], os_[0], src[0]), [src], [oq, os_])
+
+    def mm(ps, bank, lq, ls, la, rq, rs, a, b):
+        out = view(ps, 512 * bank, 512 * bank + b - a)
+        l0, l1, r0, r1 = view(lq, la, la + 128), view(ls, la, la + 128), view(rq, a, b), view(rs, a, b)
+        op("t", "c", lambda: g.tensor.matmul_mx(out[0], l0[0], l1[0], r0[0], r1[0], True, True), [l0, l1, r0, r1], [out])
+
+    def col(name, c, n=1):
+        return view(name, c, c + n)
+
+    peers = [T.cores[(rank + s) % len(T.cores)] for s in STEP]
+    mask = topo.mask(core, peers[0])
+    for p in peers:
+        mask &= topo.mask(core, p)
+    nen = bin(mask).count("1")
+
+    def send(t):
+        rid, pid = topo.addr(peers[t], core)
+        arr = T.sem["arr%d" % t]
+        cq, cs = view("gq%d" % t, 0, H), view("gs%d" % t, 0, H)
+        op("g", "remote", lambda: g.remote_dma(T["lq%d" % t][:, 0:H].bitcast(dt.uint8), cq[0].bitcast(dt.uint8),
+                                               arr, T.sem.sent, pid, rid, mask), [cq], [])
+        op("g", "remote", lambda: g.remote_dma(T["ls%d" % t][:, 0:H], cs[0], arr, T.sem.sent, pid, rid, mask), [cs], [])
+
+    def arrival(t):
+        op(None, "arrive", ("arr%d" % t, 2 * nen), [], [view("lq%d" % t, 0, H), view("ls%d" % t, 0, H)])
+
+    njunk = [0]
+
+    def count(t, base, top, out):
+        j = njunk[0]
+        njunk[0] += 1
+        act(view("junk", H * j, H * j + H), view("run%d" % t, base, base + H), ACT.Sign, scale=-1.0,
+            bias=col("run%d" % t, top), acc=out)
+
+    dma("s", view("ut", 0, 512), T.u[:, 0:512])
+    dma("y", view("xt0", 4 * H, 4 * C), T.x[:, 4 * H:4 * C])
+    dma("s", view("coi", 0, 20), T.co[:, 0:20])
+    dma("y", view("xt0", 0, 4 * H), T.x[:, 0:4 * H])
+    dma("s", view("sg", 0, 8), T.bm[:, 0:8])
+    dma("y", view("cni", 0, 30), T.cn[:, 0:30])
+    dma("s", view("bt", 0, 4 * C), T.bm[:, 0:4 * C])
+    dma("y", bits(view("wq", 0, 512)), T.wc[:, 0:2048], after=col("xt0", 0))
+    dma("y", view("wp", 0, 512), T.ws[:, 0:512])
+
+    fill(view("ones", 0, 128), 1.0)
+    o_ = view("uli", 0, 8)
+    op("g", "c", lambda: g.iota(o_[0], [[16, 8]], 0, 0), [], [o_])
+    i_, n_ = view("idn", 0, 128), view("ones", 0, 128)
+    op("g", "c", lambda: g.affine_select(i_[0], n_[0], [[-1, 128]], ALU.is_equal, 0.0, 0, 1), [n_], [i_])
+    r_ = view("ramp", 0, C)
+    op("g", "c", lambda: g.iota(r_[0], [[1, C]], 0, 0, allow_small_or_imprecise_dtypes=True), [], [r_])
+    fill(view("em", 0, 528), 0.0)
+    fill(view("sg", 8, 512), 0.0)
+    fill(view("dm", 0, H), LOW)
+    copy(view("ul16", 0, 8), view("uli", 0, 8))
+    copy(view("em", 3, 515, 4), view("idn", 0, 128))
+    for b in range(4):
+        quant("qe", "se", 128 * b, 128 * b + 128, "em", 3 - b)
+
+    def peak1_a(t):
+        scan(view("run%d" % t, 176, 336), view("pd", 3 * 512, 3 * 512 + H), view("dm", 0, H))
+        count(t, 176, 335, col("olb", 2 * t + 1))
+        act(col("dm", H), col("run%d" % t, 335), ACT.Copy)
+        if t:
+            bundle("low%d" % (t - 1))
+
+    def peak1_b(t):
+        copy(col("of%d" % t, OK1), col("olb", 2 * t + 1))
+        act(view("tab", H, H + 16), pickv(view("tab", 176, 336), col("of%d" % t, OK1)), ACT.Copy)
+
+    def peak1_c(t):
+        act(view("sm%d" % t, SE1, SE1 + 10), view("cof", 10, 20), ACT.Abs, scale=-1.0, bias=col("tab", H))
+        if t:
+            bundle("low%d" % (t - 1))
+
+    def scan0(t):
+        scan(view("run%d" % t, 0, H + 1), view("pr", 0, H + 1), view("dm", 0, H + 1))
+
+    def count_h(t):
+        count(t, 0, H, col("sm%d" % t, SH))
+
+    def count_0(t):
+        count(t, 0, H - 1, col("sm%d" % t, SK0))
+
+    def list_h(t):
+        copy(view("of%d" % t, OE1, OH + 1), view("sm%d" % t, SE1, SH + 1))
+
+    def far(t):
+        act(view("sm%d" % t, SAH, SAH + 16), pickv(view("tab", 0, H + 1), col("of%d" % t, OH)), ACT.Copy)
+        act(view("sm%d" % t, SD, SD + 10), view("cnf", 10 * t, 10 * t + 10), ACT.Abs, scale=-1.0, bias=col("sm%d" % t, SAH))
+
+    def sign(t):
+        ts(col("sm%d" % t, SC), col("pr", 512), 0.0, 0.5, ALU.is_gt, ALU.subtract)
+
+    def beam(t, b, a):
+        tt(view("z%d" % t, C * b + a, C * b + a + H), view("pr" if a else "pd", 512 * b, 512 * b + H),
+           view("zh%d" % (t - 1), C * b + a, C * b + a + H), ALU.add)
+
+    def plane(t, b, a=0, n=C):
+        if t == 0:
+            return view("bt", 4 * a + b, 4 * (a + n), 4)
+        return view("z%d" % t, C * b + a, C * b + a + n)
+
+    def tail(t):
+        sm, of, gt = "sm%d" % t, "of%d" % t, "gt%d" % t
+        if t == 0:
+            for b in (0, 2, 1, 3):
+                ts(view(of, OG4 + 10 * b, OG4 + 10 * b + 10), view(sm, SD, SD + 10), 4.0, float(b), ALU.mult, ALU.add)
+            src = [pickv(view("bt", 0, 4 * C), view(of, OG4 + 10 * b, OG4 + 10 * b + 10)) for b in range(4)]
+            for b in (0, 1):
+                act(view(gt, b, 4 * H, 4), src[b], ACT.Copy, scale=col(sm, SC))
+            for b in (2, 3):
+                ts(view(gt, b, 4 * H, 4), src[b], col(sm, SC), None, ALU.mult)
+        else:
+            src = [pickv(view("z%d" % t, C * b, C * b + C), view(of, OG, OG + 10)) for b in range(4)]
+            for b in (0, 1):
+                act(view(gt, b, 4 * H, 4), src[b], ACT.Copy, scale=col(sm, SCS))
+            for b in (2, 3):
+                ts(view(gt, b, 4 * H, 4), src[b], col(sm, SC), 1.0 / 64, ALU.mult, ALU.mult)
+        quant("gq%d" % t, "gs%d" % t, 0, H, gt, 0)
+        send(t)
+
+    def window(t):
+        sm, of, cb, xo, xn = "sm%d" % t, "of%d" % t, "cb%d" % t, "xt%d" % t, "xt%d" % (t + 1)
+        q1, s1 = "qx%d" % (t + 1), "sx%d" % (t + 1)
+        last = t == R - 1
+        back = -1.0 if t == 0 else -1.0 / 64
+
+        def e1(b):
+            tt(view(xn, 4 * H + b, 4 * C, 4), pickv(view(cb, C * b, C * b + C), view(of, OE1, OE1 + 10)),
+               view(xo, 4 * H + b, 4 * C, 4), ALU.add)
+
+        def e0(b):
+            tt(view("e%d" % t, H * b, H * b + H), pickv(view(cb, C * b, C * b + C), view(of, OE0, OE0 + 10)),
+               view(xo, b, 4 * H, 4), ALU.add)
+            bundle("e%d" % t)
+
+        def neg(b):
+            act(view(cb, C * b, C * b + C), plane(t, b), ACT.Copy, scale=col(sm, SCN))
+
+        def half(b, a):
+            act(view("zh%d" % t, C * b + a, C * b + a + H), plane(t, b, a, H), ACT.Copy, scale=32.0 if t == 0 else 0.5)
+            bundle(("high%d" if a else "low%d") % t)
+
+        def q_1():
+            quant(q1, s1, H, C, xn, 4 * H)
+            if not last:
+                mm("pd", 3, "qup", "sup", 0, q1, s1, H, C)
+                for b in range(4):
+                    mm("pr", b, "wq", "wp", 128 * b, q1, s1, H, C)
+                    bundle("high%d" % t)
+
+        if t == 0:
+            copy(col(of, OK0), col(sm, SK0))
+        ts(view(cb, 0, C), plane(t, 0), col(sm, SC), back, ALU.mult, ALU.mult)
+        act(col(sm, SCN), col(sm, SC), ACT.Copy, scale=back)
+        act(view(sm, SA0, SA0 + 16), pickv(view("tab", 0, H), col(of, OK0)), ACT.Copy)
+        neg(1)
+        act(view(sm, SE0, SE0 + 10), view("cof", 0, 10), ACT.Abs, scale=-1.0, bias=col(sm, SA0))
+        neg(2)
+        neg(3)
+        steps = {"a": lambda: e1(0), "b": lambda: e1(1), "c": lambda: e1(2), "d": lambda: e1(3), "q": q_1,
+                 "l": lambda: copy(view(of, OE0, OE0 + 10), view(sm, SE0, SE0 + 10)),
+                 "0": lambda: e0(0), "1": lambda: e0(1), "2": lambda: e0(2), "3": lambda: e0(3),
+                 "s": lambda: peak1_a(t + 1), "k": lambda: peak1_b(t + 1), "n": lambda: peak1_c(t + 1),
+                 "h": lambda: [half(b, H) for b in range(4)], "g": lambda: [half(b, 0) for b in range(4)],
+                 "w": lambda: beam(t + 1, 0, H), "x": lambda: beam(t + 1, 1, H),
+                 "y": lambda: beam(t + 1, 2, H), "z": lambda: beam(t + 1, 3, H)}
+        for ch in ORDER["last" if last else "window"]:
+            steps[ch]()
+        if last:
+            dma("y", T.oc[:, 4 * H:4 * C], bits(view(q1, H, C)))
+            quant("qv", "sv", 0, 128, "vt", 0)
+            mm("pr", 0, "qv", "sv", 0, q1, s1, H, C)
+            act(view("olf", 1, 6, 2), view("olb", 1, 6, 2), ACT.Identity, bias=float(H))
+            for r in range(R):
+                act(col("olf", 2 * r), col("sm%d" % r, SK0), ACT.Copy)
+            dma("y", T.ol[0:8, 0:6], (T.olf[0:128:16, 0:6], view("olf", 0, 6)[1]))
+            act(view("ysb", H, C), view("pr", 0, H), ACT.Copy)
+            dma("s", T.y[:, H:C], view("ysb", H, C))
+
+    def landed(t):
+        arrival(t)
+        for b in range(4):
+            mm("pd", b, "qe", "se", 128 * b, "lq%d" % t, "ls%d" % t, 0, H)
+            tt(view("xt%d" % (t + 1), b, 4 * H, 4), view("e%d" % t, H * b, H * b + H),
+               view("pd", 512 * b, 512 * b + H), ALU.subtract)
+        quant("qx%d" % (t + 1), "sx%d" % (t + 1), 0, H, "xt%d" % (t + 1), 0)
+
+    def chain(t):
+        q, s, sm, of = "qx%d" % t, "sx%d" % t, "sm%d" % t, "of%d" % t
+        landed(t - 1)
+        if t == 1:
+            dma("y", view("vt", 0, 512), T.v[:, 0:512], after=col("lq0", 0))
+        mm("pr", 0, "qup", "sup", 0, q, s, 0, H + 2)
+        for b in range(4):
+            mm("pd", b, "wq", "wp", 128 * b, q, s, 0, H)
+
+        def first():
+            tt(view("sg", 0, 4), view("pd", 0, 1537, 512), view("zh%d" % (t - 1), 0, 3 * C + 1, C), ALU.add)
+
+        def score():
+            quant("qs%d" % t, "ss%d" % t, 0, 128, "sg", 0)
+            mm("pr", 1, "qup", "sup", 0, "qs%d" % t, "ss%d" % t, 0, 128)
+
+        def signs():
+            sign(t)
+            act(col(sm, SCS), col(sm, SC), ACT.Copy, scale=1.0 / 64)
+
+        steps = {"s": lambda: scan0(t), "h": lambda: count_h(t), "k": lambda: count_0(t), "l": lambda: list_h(t),
+                 "f": lambda: far(t), "c": first, "q": score, "g": signs,
+                 "o": lambda: copy(view(of, OG, OK0 + 1), view(sm, SD, SK0 + 1)),
+                 "Y": lambda: beam(t, 2, H), "Z": lambda: beam(t, 3, H),
+                 "0": lambda: beam(t, 0, 0), "1": lambda: beam(t, 1, 0), "2": lambda: beam(t, 2, 0), "3": lambda: beam(t, 3, 0)}
+        for ch in ORDER["chain"]:
+            steps[ch]()
+
+    quant("qu", "su", 0, 128, "ut", 0)
+    pq_o, pq_i, pl = view("qup", 0, 128), view("qu", 0, 128), view("ul16", 0, 8)
+    op("v", "c", lambda: g.vector.tensor_copy(pq_o[0].bitcast(dt.uint32), pq_i[0].bitcast(dt.uint32).indirect(pl[0])),
+       [pq_i, pl], [pq_o])
+    act(view("sup", 0, 128), pickv(view("su", 0, 128), pl), ACT.Copy)
+    quant("qx0", "sx0", H, C, "xt0", 4 * H)
+    mm("pd", 3, "qup", "sup", 0, "qx0", "sx0", H, C)
+    copy(view("co16", 0, 20), view("coi", 0, 20))
+    act(view("tab", 176, 336), pickv(view("ramp", 0, C), view("co16", 10, 20)), ACT.Copy)
+    peak1_a(0)
+    act(view("tab", 0, H), pickv(view("ramp", 0, C), view("co16", 0, 10)), ACT.Copy)
+    copy(view("cof", 0, 20), view("coi", 0, 20))
+    quant("qx0", "sx0", 0, H, "xt0", 0)
+    mm("pr", 0, "qup", "sup", 0, "qx0", "sx0", 0, H + 2)
+    peak1_b(0)
+    scan0(0)
+    peak1_c(0)
+    count_h(0)
+    quant("qs0", "ss0", 0, 128, "sg", 0)
+    mm("pr", 1, "qup", "sup", 0, "qs0", "ss0", 0, 128)
+    count_0(0)
+    list_h(0)
+    copy(view("cnf", 0, 30), view("cni", 0, 30))
+    far(0)
+    sign(0)
+    tail(0)
+    window(0)
+
+    for t in range(1, R):
+        chain(t)
+        tail(t)
+        window(t)
+
+    landed(R - 1)
+    q, s = "qx%d" % R, "sx%d" % R
+    mm("pr", 1, "qv", "sv", 0, q, s, 0, H)
+    dma("y", T.oc[:, 0:4 * H], bits(view(q, 0, H)))
+    copy(view("ysb", 0, H), view("pr", 512, 512 + H))
+    for k in range(4):
+        if k == 3:
+            dma("s", T.y[:, 0:H], view("ysb", 0, H))
+        dma("y" if k < 2 else "s", T.osc[4 * k:4 * k + 4, 0:C], (T[s][32 * k:32 * k + 4, 0:C], view(s, 0, C)[1]))
+    return ops, Q, 2 * R * nen
+
+
+def clash(a, b):
+    for n1, m1 in a:
+        for n2, m2 in b:
+            if n1 == n2 and m1 & m2:
+                return True
+    return False
+
+
+def order(ops):
+    known, seen, waits = {}, [], []
+    for i, o in enumerate(ops):
+        ps_i = [x for x in o["rd"] if x[0] in ("pd", "pr")]
+        have = known.get(o["q"], 0) if o["q"] else 0
+        need = []
+        for j in range(i):
+            p = ops[j]
+            if have >> j & 1 or p["kind"] == "remote" or o["kind"] == "arrive":
+                continue
+            if clash(o["rd"], p["wr"]) or clash(o["wr"], p["wr"]) or clash(o["wr"], p["rd"]) or (
+                    p["q"] != o["q"] and clash(ps_i, p["rd"])):
+                need.append(j)
+        sets = [ops[j]["set"] for j in need if ops[j]["set"]]
+        need += [j for j in range(i) if ops[j]["set"] in sets and j not in need and not have >> j & 1]
+        implied = 0
+        for j in need:
+            implied |= seen[j]
+        need = [j for j in need if not implied >> j & 1]
+        for j in need:
+            have |= seen[j] | 1 << j
+        if o["q"]:
+            known[o["q"]] = have
+        seen.append(have)
+        waits.append(need)
+    return waits, seen
+
+
+def rank_program(g, core, T, topo):
+    rank = T.rank_of(core)
+    if rank is None:
+        return
+    ops, Q, sent = build(g, core, T, topo, rank)
+    waits, seen = order(ops)
+    n = len(ops)
+    tails = {}
+    for j, o in enumerate(ops):
+        if o["kind"] == "dma" and not o["wr"]:
+            tails.setdefault(o["q"], []).append(j)
+    ends = sorted(tails)
+    for q in ends:
+        waits.append(tails[q])
+    waiters = {}
+    for i, w in enumerate(waits):
+        for j in w:
+            waiters.setdefault(j, []).append(i)
+
+    def queue(i):
+        return ops[i]["q"] if i < n else ends[i - n]
+
+    rides = {}
+    for j in sorted(waiters, reverse=True):
+        if ops[j]["kind"] != "c":
+            continue
+        for k in range(j + 1, waiters[j][0]):
+            if k in waiters and k not in rides and ops[k]["kind"] == "c" and ops[k]["q"] == ops[j]["q"] and all(
+                    any(queue(m) == queue(i) and m <= i for m in waiters[k]) for i in waiters[j]):
+                rides[j] = k
+                break
+    for j in rides:
+        for i in waiters[j]:
+            waits[i].remove(j)
+    groups, home = {}, {}
+    for j in sorted(waiters):
+        if ops[j]["kind"] != "arrive" and j not in rides:
+            home[j] = (ops[j]["kind"], tuple(waiters[j]))
+            groups.setdefault(home[j], []).append(j)
+    for j in sorted(rides):
+        groups[home[rides[j]]].append(j)
+    token, pool = {}, []
+    for key in sorted(groups, key=lambda k: min(groups[k])):
+        mem = groups[key]
+        inc = 16 if key[0] == "dma" else 1
+        slot = None
+        if len(pool) < NPOOL:
+            slot = {"name": "s%d" % len(pool), "kind": key[0], "count": 0, "last": []}
+            pool.append(slot)
+        else:
+            for sl in pool:
+                if sl["kind"] == key[0] and all(seen[m] >> j & 1 for m in mem for j in sl["last"]):
+                    slot = sl
+                    break
+        slot["count"] += inc * len(mem)
+        slot["last"] = mem
+        for j in mem:
+            token[j] = (slot["name"], slot["count"], inc)
+    for j, o in enumerate(ops):
+        if o["kind"] == "arrive":
+            token[j] = (o["fn"][0], o["fn"][1], 0)
+
+    def wait(q, js):
+        done = []
+        for j in js:
+            tk = token[j][:2]
+            if tk not in done:
+                done.append(tk)
+                Q[q].wait_ge(T.sem[tk[0]], tk[1])
+
+    for i, o in enumerate(ops):
+        if o["kind"] == "arrive":
+            continue
+        wait(o["q"], waits[i])
+        ins = o["fn"]()
+        if i in token:
+            ins.then_inc(T.sem[token[i][0]], token[i][2])
+    for k, q in enumerate(ends):
+        wait(q, waits[n + k])
+    g.wait_ge(T.sem.sent, sent)

@@ -52,7 +52,18 @@ SEMAPHORES = ["sent", "arr0", "arr1", "arr2"] + ["s%d" % _i for _i in range(NPOO
 ALU, ACT = AluOpType, ActivationFunctionType
 SC, SCS, SCN, SD, SK0, SE1, SH, SE0, SAH, SA0 = 0, 1, 2, 16, 26, 32, 42, 48, 64, 80
 OG, OK0, OE1, OH, OE0, OK1, OG4 = 0, 10, 12, 22, 24, 34, 36
-ORDER = {"chain": "Zsh01clqkf2go3", "window": "abclhdq0s1k2n3gwxy", "last": "al0b1c2d3q"}
+
+LOADS = [("s", "u"), ("y", "x1 x0 co b0 cn bm wc ws")]
+ORDER = {
+    "first": "zeros unit0 unit1 qu picku picks q1 scan1 count1 best1 q0 co16 tab0 list1 scan0 tab1v counth at1 score onlyh cnf ath "
+             "sign farh count0 lists0 lists2 tail0 lists1 lists3 tail2 tail1 back tail3 cof send far1 onlyk only1 negv0",
+    "chain": "q0 high2 high3 scan0 beam0 counth beam1 col0 listh count0 score ath beam2 farh sign listg fore back "
+             "tail0 beam3 tail2 tail1 tail3 negv0 send",
+    "window": "neg1 neg2 neg3 at0 far0 e1_0 e1_1 e1_2 e1_3 list0 half0 q1+ e0_0 e0_1 scan1+ half1 count1+ best1+ "
+              "e0_2 half2 e0_3 high0+ list1+ at1+ high1+ far1+ half3 keep0",
+    "spare": "unit2 unit3",
+    "last": "neg1 neg2 neg3 at0 far0 e1_0 e1_1 e1_2 e1_3 list0 q1+ e0_0 e0_1 e0_2 e0_3 keep0 peaks out1",
+}
 
 
 def build(g, core, T, topo, rank):
@@ -141,30 +152,24 @@ def build(g, core, T, topo, rank):
         rid, pid = topo.addr(peers[t], core)
         arr = T.sem["arr%d" % t]
         cq, cs = view("gq%d" % t, 0, H), view("gs%d" % t, 0, H)
+        quant("gq%d" % t, "gs%d" % t, 0, H, "gt%d" % t, 0)
         op("g", "remote", lambda: g.remote_dma(T["lq%d" % t][:, 0:H].bitcast(dt.uint8), cq[0].bitcast(dt.uint8),
                                                arr, T.sem.sent, pid, rid, mask), [cq], [])
         op("g", "remote", lambda: g.remote_dma(T["ls%d" % t][:, 0:H], cs[0], arr, T.sem.sent, pid, rid, mask), [cs], [])
 
-    def arrival(t):
-        op(None, "arrive", ("arr%d" % t, 2 * nen), [], [view("lq%d" % t, 0, H), view("ls%d" % t, 0, H)])
-
-    njunk = [0]
-
-    def count(t, base, top, out):
-        j = njunk[0]
-        njunk[0] += 1
-        act(view("junk", H * j, H * j + H), view("run%d" % t, base, base + H), ACT.Sign, scale=-1.0,
-            bias=col("run%d" % t, top), acc=out)
-
-    dma("s", view("ut", 0, 512), T.u[:, 0:512])
-    dma("y", view("xt0", 4 * H, 4 * C), T.x[:, 4 * H:4 * C])
-    dma("s", view("coi", 0, 20), T.co[:, 0:20])
-    dma("y", view("xt0", 0, 4 * H), T.x[:, 0:4 * H])
-    dma("s", view("sg", 0, 8), T.bm[:, 0:8])
-    dma("y", view("cni", 0, 30), T.cn[:, 0:30])
-    dma("s", view("bt", 0, 4 * C), T.bm[:, 0:4 * C])
-    dma("y", bits(view("wq", 0, 512)), T.wc[:, 0:2048], after=col("xt0", 0))
-    dma("y", view("wp", 0, 512), T.ws[:, 0:512])
+    loads = {"u": lambda q: dma(q, view("ut", 0, 512), T.u[:, 0:512]),
+             "x1": lambda q: dma(q, view("xt0", 4 * H, 4 * C), T.x[:, 4 * H:4 * C]),
+             "x0": lambda q: dma(q, view("xt0", 0, 4 * H), T.x[:, 0:4 * H]),
+             "x": lambda q: dma(q, view("xt0", 0, 4 * C), T.x[:, 0:4 * C]),
+             "co": lambda q: dma(q, view("coi", 0, 20), T.co[:, 0:20]),
+             "cn": lambda q: dma(q, view("cni", 0, 30), T.cn[:, 0:30]),
+             "b0": lambda q: dma(q, view("sg", 0, 8), T.bm[:, 0:8]),
+             "bm": lambda q: dma(q, view("bt", 0, 4 * C), T.bm[:, 0:4 * C]),
+             "wc": lambda q: dma(q, bits(view("wq", 0, 512)), T.wc[:, 0:2048], after=col("xt0", 0)),
+             "ws": lambda q: dma(q, view("wp", 0, 512), T.ws[:, 0:512])}
+    for q, names in LOADS:
+        for name in names.split():
+            loads[name](q)
 
     fill(view("ones", 0, 128), 1.0)
     o_ = view("uli", 0, 8)
@@ -174,81 +179,80 @@ def build(g, core, T, topo, rank):
     r_ = view("ramp", 0, C)
     op("g", "c", lambda: g.iota(r_[0], [[1, C]], 0, 0, allow_small_or_imprecise_dtypes=True), [], [r_])
     fill(view("em", 0, 528), 0.0)
-    fill(view("sg", 8, 512), 0.0)
     fill(view("dm", 0, H), LOW)
     copy(view("ul16", 0, 8), view("uli", 0, 8))
     copy(view("em", 3, 515, 4), view("idn", 0, 128))
-    for b in range(4):
-        quant("qe", "se", 128 * b, 128 * b + 128, "em", 3 - b)
 
-    def peak1_a(t):
-        scan(view("run%d" % t, 176, 336), view("pd", 3 * 512, 3 * 512 + H), view("dm", 0, H))
-        count(t, 176, 335, col("olb", 2 * t + 1))
-        act(col("dm", H), col("run%d" % t, 335), ACT.Copy)
-        if t:
-            bundle("low%d" % (t - 1))
+    njunk = [0]
 
-    def peak1_b(t):
-        copy(col("of%d" % t, OK1), col("olb", 2 * t + 1))
-        act(view("tab", H, H + 16), pickv(view("tab", 176, 336), col("of%d" % t, OK1)), ACT.Copy)
-
-    def peak1_c(t):
-        act(view("sm%d" % t, SE1, SE1 + 10), view("cof", 10, 20), ACT.Abs, scale=-1.0, bias=col("tab", H))
-        if t:
-            bundle("low%d" % (t - 1))
-
-    def scan0(t):
-        scan(view("run%d" % t, 0, H + 1), view("pr", 0, H + 1), view("dm", 0, H + 1))
-
-    def count_h(t):
-        count(t, 0, H, col("sm%d" % t, SH))
-
-    def count_0(t):
-        count(t, 0, H - 1, col("sm%d" % t, SK0))
-
-    def list_h(t):
-        copy(view("of%d" % t, OE1, OH + 1), view("sm%d" % t, SE1, SH + 1))
-
-    def far(t):
-        act(view("sm%d" % t, SAH, SAH + 16), pickv(view("tab", 0, H + 1), col("of%d" % t, OH)), ACT.Copy)
-        act(view("sm%d" % t, SD, SD + 10), view("cnf", 10 * t, 10 * t + 10), ACT.Abs, scale=-1.0, bias=col("sm%d" % t, SAH))
-
-    def sign(t):
-        ts(col("sm%d" % t, SC), col("pr", 512), 0.0, 0.5, ALU.is_gt, ALU.subtract)
-
-    def beam(t, b, a):
-        tt(view("z%d" % t, C * b + a, C * b + a + H), view("pr" if a else "pd", 512 * b, 512 * b + H),
-           view("zh%d" % (t - 1), C * b + a, C * b + a + H), ALU.add)
-
-    def plane(t, b, a=0, n=C):
-        if t == 0:
-            return view("bt", 4 * a + b, 4 * (a + n), 4)
-        return view("z%d" % t, C * b + a, C * b + a + n)
-
-    def tail(t):
-        sm, of, gt = "sm%d" % t, "of%d" % t, "gt%d" % t
-        if t == 0:
-            for b in (0, 2, 1, 3):
-                ts(view(of, OG4 + 10 * b, OG4 + 10 * b + 10), view(sm, SD, SD + 10), 4.0, float(b), ALU.mult, ALU.add)
-            src = [pickv(view("bt", 0, 4 * C), view(of, OG4 + 10 * b, OG4 + 10 * b + 10)) for b in range(4)]
-            for b in (0, 1):
-                act(view(gt, b, 4 * H, 4), src[b], ACT.Copy, scale=col(sm, SC))
-            for b in (2, 3):
-                ts(view(gt, b, 4 * H, 4), src[b], col(sm, SC), None, ALU.mult)
-        else:
-            src = [pickv(view("z%d" % t, C * b, C * b + C), view(of, OG, OG + 10)) for b in range(4)]
-            for b in (0, 1):
-                act(view(gt, b, 4 * H, 4), src[b], ACT.Copy, scale=col(sm, SCS))
-            for b in (2, 3):
-                ts(view(gt, b, 4 * H, 4), src[b], col(sm, SC), 1.0 / 64, ALU.mult, ALU.mult)
-        quant("gq%d" % t, "gs%d" % t, 0, H, gt, 0)
-        send(t)
-
-    def window(t):
-        sm, of, cb, xo, xn = "sm%d" % t, "of%d" % t, "cb%d" % t, "xt%d" % t, "xt%d" % (t + 1)
-        q1, s1 = "qx%d" % (t + 1), "sx%d" % (t + 1)
-        last = t == R - 1
+    def steps(t):
+        sm, of, cb, gt, run = "sm%d" % t, "of%d" % t, "cb%d" % t, "gt%d" % t, "run%d" % t
+        xo, xn, q, s = "xt%d" % t, "xt%d" % (t + 1), "qx%d" % t, "sx%d" % t
         back = -1.0 if t == 0 else -1.0 / 64
+
+        def count(base, top, out):
+            j = njunk[0]
+            njunk[0] += 1
+            act(view("junk", H * j, H * j + H), view(run, base, base + H), ACT.Sign, scale=-1.0, bias=col(run, top), acc=out)
+
+        def plane(b, a=0, n=C):
+            if t == 0:
+                return view("bt", 4 * a + b, 4 * (a + n), 4)
+            return view("z%d" % t, C * b + a, C * b + a + n)
+
+        def q1():
+            quant(q, s, H, C, xo, 4 * H)
+            if t < R:
+                mm("pd", 3, "qup", "sup", 0, q, s, H, C)
+            if 0 < t < R:
+                for b in range(4):
+                    mm("pr", b, "wq", "wp", 128 * b, q, s, H, C)
+
+        def q0():
+            quant(q, s, 0, H, xo, 0)
+            if t < R:
+                mm("pr", 0, "qup", "sup", 0, q, s, 0, H + 2)
+            if 0 < t < R:
+                for b in range(4):
+                    mm("pd", b, "wq", "wp", 128 * b, q, s, 0, H)
+
+        def landed():
+            lq, ls = "lq%d" % (t - 1), "ls%d" % (t - 1)
+            op(None, "arrive", ("arr%d" % (t - 1), 2 * nen), [], [view(lq, 0, H), view(ls, 0, H)])
+            for b in range(4):
+                mm("pd", b, "qe", "se", 128 * b, lq, ls, 0, H)
+                tt(view(xo, b, 4 * H, 4), view("e%d" % (t - 1), H * b, H * b + H), view("pd", 512 * b, 512 * b + H), ALU.subtract)
+
+        def picku():
+            o, i, l = view("qup", 0, 128), view("qu", 0, 128), view("ul16", 0, 8)
+            op("v", "c", lambda: g.vector.tensor_copy(o[0].bitcast(dt.uint32), i[0].bitcast(dt.uint32).indirect(l[0])), [i, l], [o])
+
+        def score():
+            quant("qs%d" % t, "ss%d" % t, 0, 128, "sg", 0)
+            mm("pr", 0, "qup", "sup", 0, "qs%d" % t, "ss%d" % t, 0, 128)
+
+        def beam(b, a):
+            tt(view("z%d" % t, C * b + a, C * b + a + H), view("pr" if a else "pd", 512 * b, 512 * b + H),
+               view("zh%d" % (t - 1), C * b + a, C * b + a + H), ALU.add)
+
+        def tail(b):
+            if t == 0:
+                src = pickv(view("bt", 0, 4 * C), view(of, OG4 + 10 * b, OG4 + 10 * b + 10))
+            else:
+                src = pickv(plane(b), view(of, OG, OG + 10))
+            if b < 2:
+                act(view(gt, b, 4 * H, 4), src, ACT.Copy, scale=col(sm, SCS if t else SC))
+            else:
+                ts(view(gt, b, 4 * H, 4), src, col(sm, SC), -back, ALU.mult, ALU.mult)
+
+        def lists(b):
+            ts(view(of, OG4 + 10 * b, OG4 + 10 * b + 10), view(sm, SD, SD + 10), 4.0, float(b), ALU.mult, ALU.add)
+
+        def neg(b, vec):
+            if vec:
+                ts(view(cb, C * b, C * b + C), plane(b), col(sm, SC), back, ALU.mult, ALU.mult)
+            else:
+                act(view(cb, C * b, C * b + C), plane(b), ACT.Copy, scale=col(sm, SCN))
 
         def e1(b):
             tt(view(xn, 4 * H + b, 4 * C, 4), pickv(view(cb, C * b, C * b + C), view(of, OE1, OE1 + 10)),
@@ -257,130 +261,96 @@ def build(g, core, T, topo, rank):
         def e0(b):
             tt(view("e%d" % t, H * b, H * b + H), pickv(view(cb, C * b, C * b + C), view(of, OE0, OE0 + 10)),
                view(xo, b, 4 * H, 4), ALU.add)
-            bundle("e%d" % t)
 
-        def neg(b):
-            act(view(cb, C * b, C * b + C), plane(t, b), ACT.Copy, scale=col(sm, SCN))
+        def half(b):
+            act(view("zh%d" % t, C * b, C * b + C), plane(b), ACT.Copy, scale=32.0 if t == 0 else 0.5)
 
-        def half(b, a):
-            act(view("zh%d" % t, C * b + a, C * b + a + H), plane(t, b, a, H), ACT.Copy, scale=32.0 if t == 0 else 0.5)
-            bundle(("high%d" if a else "low%d") % t)
-
-        def q_1():
-            quant(q1, s1, H, C, xn, 4 * H)
-            if not last:
-                mm("pd", 3, "qup", "sup", 0, q1, s1, H, C)
-                for b in range(4):
-                    mm("pr", b, "wq", "wp", 128 * b, q1, s1, H, C)
-                    bundle("high%d" % t)
-
-        if t == 0:
-            copy(col(of, OK0), col(sm, SK0))
-        ts(view(cb, 0, C), plane(t, 0), col(sm, SC), back, ALU.mult, ALU.mult)
-        act(col(sm, SCN), col(sm, SC), ACT.Copy, scale=back)
-        act(view(sm, SA0, SA0 + 16), pickv(view("tab", 0, H), col(of, OK0)), ACT.Copy)
-        neg(1)
-        act(view(sm, SE0, SE0 + 10), view("cof", 0, 10), ACT.Abs, scale=-1.0, bias=col(sm, SA0))
-        neg(2)
-        neg(3)
-        steps = {"a": lambda: e1(0), "b": lambda: e1(1), "c": lambda: e1(2), "d": lambda: e1(3), "q": q_1,
-                 "l": lambda: copy(view(of, OE0, OE0 + 10), view(sm, SE0, SE0 + 10)),
-                 "0": lambda: e0(0), "1": lambda: e0(1), "2": lambda: e0(2), "3": lambda: e0(3),
-                 "s": lambda: peak1_a(t + 1), "k": lambda: peak1_b(t + 1), "n": lambda: peak1_c(t + 1),
-                 "h": lambda: [half(b, H) for b in range(4)], "g": lambda: [half(b, 0) for b in range(4)],
-                 "w": lambda: beam(t + 1, 0, H), "x": lambda: beam(t + 1, 1, H),
-                 "y": lambda: beam(t + 1, 2, H), "z": lambda: beam(t + 1, 3, H)}
-        for ch in ORDER["last" if last else "window"]:
-            steps[ch]()
-        if last:
-            dma("y", T.oc[:, 4 * H:4 * C], bits(view(q1, H, C)))
-            quant("qv", "sv", 0, 128, "vt", 0)
-            mm("pr", 0, "qv", "sv", 0, q1, s1, H, C)
-            act(view("olf", 1, 6, 2), view("olb", 1, 6, 2), ACT.Identity, bias=float(H))
-            for r in range(R):
-                act(col("olf", 2 * r), col("sm%d" % r, SK0), ACT.Copy)
-            dma("y", T.ol[0:8, 0:6], (T.olf[0:128:16, 0:6], view("olf", 0, 6)[1]))
+        def out1():
+            qn, sn = "qx%d" % R, "sx%d" % R
+            dma("y", T.oc[:, 4 * H:4 * C], bits(view(qn, H, C)))
+            mm("pr", 0, "qv", "sv", 0, qn, sn, H, C)
             act(view("ysb", H, C), view("pr", 0, H), ACT.Copy)
-            dma("s", T.y[:, H:C], view("ysb", H, C))
+            dma("y", T.y[:, H:C], view("ysb", H, C))
 
-    def landed(t):
-        arrival(t)
+        def peaks():
+            act(view("olf", 1, 6, 2), view("olb", 1, 6, 2), ACT.Identity, bias=float(H))
+            dma("y", T.ol[0:8, 0:6], (T.olf[0:128:16, 0:6], view("olf", 0, 6)[1]))
+
+        def count0():
+            count(0, H - 1, col(sm, SK0))
+
+        d = {"qu": lambda: quant("qu", "su", 0, 128, "ut", 0), "qv": lambda: quant("qv", "sv", 0, 128, "vt", 0),
+             "loadv": lambda: dma("y", view("vt", 0, 512), T.v[:, 0:512], after=col("lq0", 0)),
+             "zeros": lambda: fill(view("sg", 8, 512), 0.0),
+             "picku": picku, "picks": lambda: act(view("sup", 0, 128), pickv(view("su", 0, 128), view("ul16", 0, 8)), ACT.Copy),
+             "co16": lambda: copy(view("co16", 0, 20), view("coi", 0, 20)),
+             "cof": lambda: copy(view("cof", 0, 20), view("coi", 0, 20)),
+             "cnf": lambda: copy(view("cnf", 0, 30), view("cni", 0, 30)),
+             "tab0": lambda: act(view("tab", 0, H), pickv(view("ramp", 0, C), view("co16", 0, 10)), ACT.Copy),
+             "tab1": lambda: act(view("tab", 176, 336), pickv(view("ramp", 0, C), view("co16", 10, 20)), ACT.Copy),
+             "q0": q0, "q1": q1, "landed": landed, "score": score, "send": lambda: send(t), "out1": out1, "peaks": peaks,
+             "scan1": lambda: scan(view(run, 176, 336), view("pd", 3 * 512, 3 * 512 + H), view("dm", 0, H)),
+             "count1": lambda: count(176, 335, col("olb", 2 * t + 1)),
+             "best1": lambda: act(col("dm", H), col(run, 335), ACT.Copy),
+             "list1": lambda: copy(col(of, OK1), col("olb", 2 * t + 1)),
+             "at1": lambda: act(view("tab", H, H + 16), pickv(view("tab", 176, 336), col(of, OK1)), ACT.Copy),
+             "far1": lambda: act(view(sm, SE1, SE1 + 10), view("cof", 10, 20), ACT.Abs, scale=-1.0, bias=col("tab", H)),
+             "scan0": lambda: scan(view(run, 0, H + 1), view("pr", 0, H + 1), view("dm", 0, H + 1)),
+             "counth": lambda: count(0, H, col(sm, SH)),
+             "listh": lambda: copy(view(of, OE1, OH + 1), view(sm, SE1, SH + 1)),
+             "onlyh": lambda: copy(col(of, OH), col(sm, SH)),
+             "only1": lambda: copy(view(of, OE1, OE1 + 10), view(sm, SE1, SE1 + 10)),
+             "onlyg": lambda: copy(view(of, OG, OG + 10), view(sm, SD, SD + 10)),
+             "onlyk": lambda: copy(col(of, OK0), col(sm, SK0)),
+             "tab1v": lambda: copy(view("tab", 176, 336), pickv(view("ramp", 0, C), view("co16", 10, 20))),
+             "ath": lambda: act(view(sm, SAH, SAH + 16), pickv(view("tab", 0, H + 1), col(of, OH)), ACT.Copy),
+             "farh": lambda: act(view(sm, SD, SD + 10), view("cnf", 10 * t, 10 * t + 10), ACT.Abs, scale=-1.0, bias=col(sm, SAH)),
+             "listg": lambda: copy(view(of, OG, OK0 + 1), view(sm, SD, SK0 + 1)),
+             "count0": count0,
+             "keep0": lambda: act(col("olf", 2 * t), col(sm, SK0), ACT.Copy),
+             "at0": lambda: act(view(sm, SA0, SA0 + 16), pickv(view("tab", 0, H), col(of, OK0)), ACT.Copy),
+             "far0": lambda: act(view(sm, SE0, SE0 + 10), view("cof", 0, 10), ACT.Abs, scale=-1.0, bias=col(sm, SA0)),
+             "list0": lambda: copy(view(of, OE0, OE0 + 10), view(sm, SE0, SE0 + 10)),
+             "col0": lambda: tt(view("sg", 0, 4), view("pd", 0, 1537, 512), view("zh%d" % (t - 1), 0, 3 * C + 1, C), ALU.add),
+             "sign": lambda: ts(col(sm, SC), col("pr", 0), 0.0, 0.5, ALU.is_gt, ALU.subtract),
+             "fore": lambda: act(col(sm, SCS), col(sm, SC), ACT.Copy, scale=-back),
+             "back": lambda: act(col(sm, SCN), col(sm, SC), ACT.Copy, scale=back)}
         for b in range(4):
-            mm("pd", b, "qe", "se", 128 * b, "lq%d" % t, "ls%d" % t, 0, H)
-            tt(view("xt%d" % (t + 1), b, 4 * H, 4), view("e%d" % t, H * b, H * b + H),
-               view("pd", 512 * b, 512 * b + H), ALU.subtract)
-        quant("qx%d" % (t + 1), "sx%d" % (t + 1), 0, H, "xt%d" % (t + 1), 0)
+            d["unit%d" % b] = lambda b=b: quant("qe", "se", 128 * b, 128 * b + 128, "em", 3 - b)
+            d["half%d" % b] = lambda b=b: half(b)
+            d["beam%d" % b] = lambda b=b: beam(b, 0)
+            d["high%d" % b] = lambda b=b: beam(b, H)
+            d["tail%d" % b] = lambda b=b: tail(b)
+            d["lists%d" % b] = lambda b=b: lists(b)
+            d["neg%d" % b] = lambda b=b: neg(b, False)
+            d["negv%d" % b] = lambda b=b: neg(b, True)
+            d["e1_%d" % b] = lambda b=b: e1(b)
+            d["e0_%d" % b] = lambda b=b: e0(b)
+        return d
 
-    def chain(t):
-        q, s, sm, of = "qx%d" % t, "sx%d" % t, "sm%d" % t, "of%d" % t
-        landed(t - 1)
-        if t == 1:
-            dma("y", view("vt", 0, 512), T.v[:, 0:512], after=col("lq0", 0))
-        mm("pr", 0, "qup", "sup", 0, q, s, 0, H + 2)
-        for b in range(4):
-            mm("pd", b, "wq", "wp", 128 * b, q, s, 0, H)
+    S = [steps(t) for t in range(R + 1)]
 
-        def first():
-            tt(view("sg", 0, 4), view("pd", 0, 1537, 512), view("zh%d" % (t - 1), 0, 3 * C + 1, C), ALU.add)
+    def do(names, t):
+        for name in names.split():
+            S[t + 1][name[:-1]]() if name[-1] == "+" else S[t][name]()
 
-        def score():
-            quant("qs%d" % t, "ss%d" % t, 0, 128, "sg", 0)
-            mm("pr", 1, "qup", "sup", 0, "qs%d" % t, "ss%d" % t, 0, 128)
+    do(ORDER["first"], 0)
+    for t in range(R):
+        if t:
+            do("landed " + ("loadv " if t == 1 else "qv ") + ORDER["chain"], t)
+        if t < R - 1:
+            do(ORDER["window"] + ("" if t else " " + ORDER["spare"]), t)
+        else:
+            do(ORDER["last"], t)
 
-        def signs():
-            sign(t)
-            act(col(sm, SCS), col(sm, SC), ACT.Copy, scale=1.0 / 64)
-
-        steps = {"s": lambda: scan0(t), "h": lambda: count_h(t), "k": lambda: count_0(t), "l": lambda: list_h(t),
-                 "f": lambda: far(t), "c": first, "q": score, "g": signs,
-                 "o": lambda: copy(view(of, OG, OK0 + 1), view(sm, SD, SK0 + 1)),
-                 "Y": lambda: beam(t, 2, H), "Z": lambda: beam(t, 3, H),
-                 "0": lambda: beam(t, 0, 0), "1": lambda: beam(t, 1, 0), "2": lambda: beam(t, 2, 0), "3": lambda: beam(t, 3, 0)}
-        for ch in ORDER["chain"]:
-            steps[ch]()
-
-    quant("qu", "su", 0, 128, "ut", 0)
-    pq_o, pq_i, pl = view("qup", 0, 128), view("qu", 0, 128), view("ul16", 0, 8)
-    op("v", "c", lambda: g.vector.tensor_copy(pq_o[0].bitcast(dt.uint32), pq_i[0].bitcast(dt.uint32).indirect(pl[0])),
-       [pq_i, pl], [pq_o])
-    act(view("sup", 0, 128), pickv(view("su", 0, 128), pl), ACT.Copy)
-    quant("qx0", "sx0", H, C, "xt0", 4 * H)
-    mm("pd", 3, "qup", "sup", 0, "qx0", "sx0", H, C)
-    copy(view("co16", 0, 20), view("coi", 0, 20))
-    act(view("tab", 176, 336), pickv(view("ramp", 0, C), view("co16", 10, 20)), ACT.Copy)
-    peak1_a(0)
-    act(view("tab", 0, H), pickv(view("ramp", 0, C), view("co16", 0, 10)), ACT.Copy)
-    copy(view("cof", 0, 20), view("coi", 0, 20))
-    quant("qx0", "sx0", 0, H, "xt0", 0)
-    mm("pr", 0, "qup", "sup", 0, "qx0", "sx0", 0, H + 2)
-    peak1_b(0)
-    scan0(0)
-    peak1_c(0)
-    count_h(0)
-    quant("qs0", "ss0", 0, 128, "sg", 0)
-    mm("pr", 1, "qup", "sup", 0, "qs0", "ss0", 0, 128)
-    count_0(0)
-    list_h(0)
-    copy(view("cnf", 0, 30), view("cni", 0, 30))
-    far(0)
-    sign(0)
-    tail(0)
-    window(0)
-
-    for t in range(1, R):
-        chain(t)
-        tail(t)
-        window(t)
-
-    landed(R - 1)
+    do("landed q0", R)
     q, s = "qx%d" % R, "sx%d" % R
     mm("pr", 1, "qv", "sv", 0, q, s, 0, H)
     dma("y", T.oc[:, 0:4 * H], bits(view(q, 0, H)))
     copy(view("ysb", 0, H), view("pr", 512, 512 + H))
     for k in range(4):
-        if k == 3:
-            dma("s", T.y[:, 0:H], view("ysb", 0, H))
         dma("y" if k < 2 else "s", T.osc[4 * k:4 * k + 4, 0:C], (T[s][32 * k:32 * k + 4, 0:C], view(s, 0, C)[1]))
+    dma("s", T.y[:, 0:H], view("ysb", 0, H))
     return ops, Q, 2 * R * nen
 
 

@@ -3,6 +3,12 @@ from concourse.mybir import dt, AluOpType, ActivationFunctionType
 C, H, R = 320, 160, 3
 STEP = [1, 2, 4]
 LOW = -1.0e29
+TOP = H * H
+TINY = 1.0e-37
+SSIGN = True
+OWN = True
+SEEK = False
+CUT = 6
 BF, F32, I32, U16, U8, MX = "bfloat16", "float32", "int32", "uint16", "uint8", "float8_e4m3fn_x4"
 
 SCRATCH = {
@@ -19,7 +25,9 @@ SCRATCH = {
     "coi": ("sbuf", [128, 20], I32), "cof": ("sbuf", [128, 20], F32), "co16": ("sbuf", [128, 20], U16),
     "cni": ("sbuf", [128, 30], I32), "cnf": ("sbuf", [128, 30], F32),
     "ramp": ("sbuf", [128, C], F32), "tab": ("sbuf", [128, 336], F32),
-    "dm": ("sbuf", [128, 168], F32),
+    "dm": ("sbuf", [128, TOP + 8], F32),
+    "dif": ("sbuf", [128, 176], F32), "past": ("sbuf", [128, 168], F32), "sum": ("sbuf", [128, 168], F32),
+    "pi": ("sbuf", [128, 8], I32), "pm": ("sbuf", [128, 8], F32),
     "olb": ("sbuf", [128, 8], F32), "olf": ("sbuf", [128, 8], F32),
     "ysb": ("sbuf", [128, C], F32),
     "junk": ("sbuf", [128, 9 * H], BF),
@@ -31,6 +39,8 @@ for _t in range(R + 1):
 for _t in range(R):
     if _t > 0:
         SCRATCH["z%d" % _t] = ("sbuf", [128, 4 * C], BF)
+        SCRATCH["bh%d" % _t] = ("sbuf", [128, 2 * C], BF)
+        SCRATCH["dist%d" % _t] = ("sbuf", [128, 10 * H + 16], F32)
     if _t < R - 1:
         SCRATCH["zh%d" % _t] = ("sbuf", [128, 4 * C], BF)
     SCRATCH["cb%d" % _t] = ("sbuf", [128, 4 * C], BF)
@@ -42,27 +52,34 @@ for _t in range(R):
     SCRATCH["ls%d" % _t] = ("sbuf", [128, H], U8)
     SCRATCH["qs%d" % _t] = ("sbuf", [128, 128], MX)
     SCRATCH["ss%d" % _t] = ("sbuf", [128, 128], U8)
-    SCRATCH["run%d" % _t] = ("sbuf", [128, 336], F32)
+    SCRATCH["run%d" % _t] = ("sbuf", [128, 168], F32)
     SCRATCH["sm%d" % _t] = ("sbuf", [128, 96], F32)
-    SCRATCH["of%d" % _t] = ("sbuf", [128, 80], U16)
+    SCRATCH["of%d" % _t] = ("sbuf", [128, 96], U16)
 
 NPOOL = 140
 SEMAPHORES = ["sent", "arr0", "arr1", "arr2"] + ["s%d" % _i for _i in range(NPOOL)]
 
 ALU, ACT = AluOpType, ActivationFunctionType
-SC, SCS, SCN, SD, SK0, SE1, SH, SE0, SAH, SA0 = 0, 1, 2, 16, 26, 32, 42, 48, 64, 80
-OG, OK0, OE1, OH, OE0, OK1, OG4 = 0, 10, 12, 22, 24, 34, 36
+SC, SCS, SCN, SD, SK0, SE1, SH, SE0, SAH, SA0 = 0, 1, 2, 16, 30, 32, 42, 48, 64, 80
+OG, OK0, OE1, OH, OE0, OK1, OG4 = 0, 16, 18, 28, 30, 40, 42
 
-LOADS = [("s", "u"), ("y", "x1 x0 co b0 cn bm wc ws")]
+LOADS = [("s", "u"), ("y", "x1 x0 co b0 cn bm wc ws v")]
+def rows(a, b, t):
+    return " ".join("row%d@%d" % (c, t) for c in range(a, b))
+
+
+START = "back neg1 far0 neg2 neg3 e1_0 e1_1 list0 e1_2 "
+WINDOW = START + "half0 e1_3 e0_0 half1 %s q1+ e0_1 e0_2 scan1+ high0+ count1+ e0_3 high1+ %s ownh0+ ownh1+ keep0 %s"
 ORDER = {
-    "first": "zeros unit0 unit1 qu picku picks q1 scan1 count1 best1 q0 co16 tab0 list1 scan0 tab1v counth at1 score onlyh cnf ath "
-             "sign farh count0 lists0 lists2 tail0 lists1 lists3 tail2 tail1 back tail3 cof send far1 onlyk only1 negv0",
-    "chain": "q0 high2 high3 scan0 beam0 counth beam1 col0 listh count0 score ath beam2 farh sign listg fore back "
-             "tail0 beam3 tail2 tail1 tail3 negv0 send",
-    "window": "neg1 neg2 neg3 at0 far0 e1_0 e1_1 e1_2 e1_3 list0 half0 q1+ e0_0 e0_1 scan1+ half1 count1+ best1+ "
-              "e0_2 half2 e0_3 high0+ list1+ at1+ high1+ far1+ half3 keep0",
-    "spare": "unit2 unit3",
-    "last": "neg1 neg2 neg3 at0 far0 e1_0 e1_1 e1_2 e1_3 list0 q1+ e0_0 e0_1 e0_2 e0_3 keep0 peaks out1",
+    "first": "units qu unit0 picku picks q1 q0 co16 scan1 tab0 unit1 scan0 count1 tab1v list1 cnf counth at1 score count0 onlyh "
+             "unit2 cof ath signs onlyk farh lists0 lists2 lists1 lists3 fore far1 at0 tail0 tail2 tail1 tail3 negv0 send only1",
+    "chain": "list1 q0 at1 slot far1 high2 high3 scan0 beam0 counth count0 col0 beam1 ownl0 score index ownl1 beam2 pull listk "
+             "signs minus at0 beam3 tail0 tail2 tail1 tail3 negv0 send",
+    "window0": WINDOW % (rows(0, 7, 1), "halfv2 halfv3", rows(7, 10, 1) + " " + rows(0, 6, 2)),
+    "window1": WINDOW % (rows(6, 10, 2), "half2 half3", ""),
+    "late": "list1 at1 slot far1",
+    "spare": "place unit3 pm qv",
+    "last": START + "e1_3 e0_0 q1+ e0_1 e0_2 e0_3 keep0 peaks out1",
 }
 
 
@@ -116,8 +133,8 @@ def build(g, core, T, topo, rank):
         else:
             op("v", "c", lambda: g.vector.tensor_scalar(out[0], a[0], A(s1), A(s2), o0, o1), [a, s1, s2], [out])
 
-    def scan(out, d0, d1):
-        op("v", "c", lambda: g.vector.tensor_tensor_scan(out[0], d0[0], d1[0], LOW, ALU.max, ALU.max), [d0, d1], [out])
+    def scan(out, d0, d1, first=LOW, o0=ALU.max, o1=ALU.max):
+        op("v", "c", lambda: g.vector.tensor_tensor_scan(out[0], d0[0], d1[0], first, o0, o1), [d0, d1], [out])
 
     def act(out, src, func, scale=None, bias=None, acc=None):
         kw = {}
@@ -166,7 +183,8 @@ def build(g, core, T, topo, rank):
              "b0": lambda q: dma(q, view("sg", 0, 8), T.bm[:, 0:8]),
              "bm": lambda q: dma(q, view("bt", 0, 4 * C), T.bm[:, 0:4 * C]),
              "wc": lambda q: dma(q, bits(view("wq", 0, 512)), T.wc[:, 0:2048], after=col("xt0", 0)),
-             "ws": lambda q: dma(q, view("wp", 0, 512), T.ws[:, 0:512])}
+             "ws": lambda q: dma(q, view("wp", 0, 512), T.ws[:, 0:512]),
+             "v": lambda q: dma(q, view("vt", 0, 512), T.v[:, 0:512])}
     for q, names in LOADS:
         for name in names.split():
             loads[name](q)
@@ -178,22 +196,26 @@ def build(g, core, T, topo, rank):
     op("g", "c", lambda: g.affine_select(i_[0], n_[0], [[-1, 128]], ALU.is_equal, 0.0, 0, 1), [n_], [i_])
     r_ = view("ramp", 0, C)
     op("g", "c", lambda: g.iota(r_[0], [[1, C]], 0, 0, allow_small_or_imprecise_dtypes=True), [], [r_])
+    p_ = col("pi", 0)
+    op("g", "c", lambda: g.iota(p_[0], [[1, 1]], 0, 1), [], [p_])
+    fill(view("dm", 0, TOP, H), LOW)
     fill(view("em", 0, 528), 0.0)
-    fill(view("dm", 0, H), LOW)
     copy(view("ul16", 0, 8), view("uli", 0, 8))
-    copy(view("em", 3, 515, 4), view("idn", 0, 128))
+    fill(view("sg", 8, 512), 0.0)
 
     njunk = [0]
 
     def steps(t):
         sm, of, cb, gt, run = "sm%d" % t, "of%d" % t, "cb%d" % t, "gt%d" % t, "run%d" % t
         xo, xn, q, s = "xt%d" % t, "xt%d" % (t + 1), "qx%d" % t, "sx%d" % t
-        back = -1.0 if t == 0 else -1.0 / 64
+        back = (-1.0 if t == 0 else -1.0 / 64) * (0.5 if SSIGN else 1.0)
+        dist = "dist%d" % t
+        slot = "dif" if t and SEEK else "tab"
 
-        def count(base, top, out):
+        def count(name, base, top, out):
             j = njunk[0]
             njunk[0] += 1
-            act(view("junk", H * j, H * j + H), view(run, base, base + H), ACT.Sign, scale=-1.0, bias=col(run, top), acc=out)
+            act(view("junk", H * j, H * j + H), view(name, base, base + H), ACT.Sign, scale=-1.0, bias=col(name, top), acc=out)
 
         def plane(b, a=0, n=C):
             if t == 0:
@@ -240,10 +262,21 @@ def build(g, core, T, topo, rank):
                 src = pickv(view("bt", 0, 4 * C), view(of, OG4 + 10 * b, OG4 + 10 * b + 10))
             else:
                 src = pickv(plane(b), view(of, OG, OG + 10))
-            if b < 2:
-                act(view(gt, b, 4 * H, 4), src, ACT.Copy, scale=col(sm, SCS if t else SC))
+            if b < 2 and t and OWN:
+                src = pickv(view("bh%d" % t, C * b, C * b + C), view(of, OG, OG + 10))
+                act(view(gt, b, 4 * H, 4), src, ACT.Copy, scale=col(sm, SC))
+            elif b < 2:
+                act(view(gt, b, 4 * H, 4), src, ACT.Copy, scale=col(sm, SCS if t or SSIGN else SC))
             else:
                 ts(view(gt, b, 4 * H, 4), src, col(sm, SC), -back, ALU.mult, ALU.mult)
+
+        def part(vec):
+            a, n = (CUT, 10) if vec else (0, CUT)
+            out, src = view(gt, 64 * a + 1, 64 * n, 4), pickv(plane(1), view(of, OG + a, OG + n))
+            if vec:
+                ts(out, src, col(sm, SC), -back, ALU.mult, ALU.mult)
+            else:
+                act(out, src, ACT.Copy, scale=col(sm, SCS))
 
         def lists(b):
             ts(view(of, OG4 + 10 * b, OG4 + 10 * b + 10), view(sm, SD, SD + 10), 4.0, float(b), ALU.mult, ALU.add)
@@ -251,6 +284,8 @@ def build(g, core, T, topo, rank):
         def neg(b, vec):
             if vec:
                 ts(view(cb, C * b, C * b + C), plane(b), col(sm, SC), back, ALU.mult, ALU.mult)
+            elif t and b < 2:
+                act(view(cb, C * b, C * b + C), view("bh%d" % t, C * b, C * b + C), ACT.Copy, scale=col(sm, SCS))
             else:
                 act(view(cb, C * b, C * b + C), plane(b), ACT.Copy, scale=col(sm, SCN))
 
@@ -277,11 +312,13 @@ def build(g, core, T, topo, rank):
             dma("y", T.ol[0:8, 0:6], (T.olf[0:128:16, 0:6], view("olf", 0, 6)[1]))
 
         def count0():
-            count(0, H - 1, col(sm, SK0))
+            count(run, 0, H - 1, col(sm, SK0))
 
         d = {"qu": lambda: quant("qu", "su", 0, 128, "ut", 0), "qv": lambda: quant("qv", "sv", 0, 128, "vt", 0),
-             "loadv": lambda: dma("y", view("vt", 0, 512), T.v[:, 0:512], after=col("lq0", 0)),
-             "zeros": lambda: fill(view("sg", 8, 512), 0.0),
+             "tail1s": lambda: part(False), "tail1v": lambda: part(True),
+             "place": lambda: ts(col("pi", 4), col("pi", 0), 15, None, ALU.bitwise_and),
+             "pm": lambda: ts(col("pm", 0), col("pi", 4), 9.0, None, ALU.min),
+             "units": lambda: copy(view("em", 3, 515, 4), view("idn", 0, 128)),
              "picku": picku, "picks": lambda: act(view("sup", 0, 128), pickv(view("su", 0, 128), view("ul16", 0, 8)), ACT.Copy),
              "co16": lambda: copy(view("co16", 0, 20), view("coi", 0, 20)),
              "cof": lambda: copy(view("cof", 0, 20), view("coi", 0, 20)),
@@ -289,14 +326,19 @@ def build(g, core, T, topo, rank):
              "tab0": lambda: act(view("tab", 0, H), pickv(view("ramp", 0, C), view("co16", 0, 10)), ACT.Copy),
              "tab1": lambda: act(view("tab", 176, 336), pickv(view("ramp", 0, C), view("co16", 10, 20)), ACT.Copy),
              "q0": q0, "q1": q1, "landed": landed, "score": score, "send": lambda: send(t), "out1": out1, "peaks": peaks,
-             "scan1": lambda: scan(view(run, 176, 336), view("pd", 3 * 512, 3 * 512 + H), view("dm", 0, H)),
-             "count1": lambda: count(176, 335, col("olb", 2 * t + 1)),
-             "best1": lambda: act(col("dm", H), col(run, 335), ACT.Copy),
+             "scan1": lambda: scan(view("dm", TOP + 1 - H, TOP + 1), view("pd", 3 * 512, 3 * 512 + H), view("dm", 0, TOP, H)),
+             "count1": lambda: count("dm", TOP + 1 - H, TOP, col("olb", 2 * t + 1)),
              "list1": lambda: copy(col(of, OK1), col("olb", 2 * t + 1)),
-             "at1": lambda: act(view("tab", H, H + 16), pickv(view("tab", 176, 336), col(of, OK1)), ACT.Copy),
-             "far1": lambda: act(view(sm, SE1, SE1 + 10), view("cof", 10, 20), ACT.Abs, scale=-1.0, bias=col("tab", H)),
-             "scan0": lambda: scan(view(run, 0, H + 1), view("pr", 0, H + 1), view("dm", 0, H + 1)),
-             "counth": lambda: count(0, H, col(sm, SH)),
+             "at1": lambda: act(view(slot, H, H + 16), pickv(view("tab", 176, 336), col(of, OK1)), ACT.Copy),
+             "far1": lambda: act(view(sm, SE1 - 1, SE1 + 10), view("cof", 9, 20), ACT.Abs, scale=-1.0, bias=col(slot, H)),
+             "listk": lambda: copy(view(of, OK0, OE1 + 10), view(sm, SK0, SE1 + 10)),
+             "dif": lambda: tt(view("dif", 0, H - 1), view("tab", 0, H - 1), view("tab", 1, H), ALU.subtract),
+             "edge": lambda: act(col("dif", H - 1), col("dif", H), ACT.Identity, scale=-1.0, bias=col("tab", H - 1)),
+             "found": lambda: ts(view("past", 1, H + 1), view(run, 0, H), col(run, H), None, ALU.is_ge),
+             "seek": lambda: scan(view("sum", 0, H + 1), view("past", 0, H + 1), view("dif", 0, H + 1), 0.0, ALU.mult, ALU.add),
+             "none": lambda: fill(col("past", 0), 0.0),
+             "scan0": lambda: scan(view(run, 0, H + 1), view("pr", 0, H + 1), view("dm", 0, TOP + 1, H)),
+             "counth": lambda: count(run, 0, H, col(sm, SH)),
              "listh": lambda: copy(view(of, OE1, OH + 1), view(sm, SE1, SH + 1)),
              "onlyh": lambda: copy(col(of, OH), col(sm, SH)),
              "only1": lambda: copy(view(of, OE1, OE1 + 10), view(sm, SE1, SE1 + 10)),
@@ -304,8 +346,8 @@ def build(g, core, T, topo, rank):
              "onlyk": lambda: copy(col(of, OK0), col(sm, SK0)),
              "tab1v": lambda: copy(view("tab", 176, 336), pickv(view("ramp", 0, C), view("co16", 10, 20))),
              "ath": lambda: act(view(sm, SAH, SAH + 16), pickv(view("tab", 0, H + 1), col(of, OH)), ACT.Copy),
-             "farh": lambda: act(view(sm, SD, SD + 10), view("cnf", 10 * t, 10 * t + 10), ACT.Abs, scale=-1.0, bias=col(sm, SAH)),
-             "listg": lambda: copy(view(of, OG, OK0 + 1), view(sm, SD, SK0 + 1)),
+             "farh": lambda: act(view(sm, SD, SD + 10), view("cnf", 10 * t, 10 * t + 10), ACT.Abs, scale=-1.0,
+                                 bias=col("sum", H) if t and SEEK else col(sm, SAH)),
              "count0": count0,
              "keep0": lambda: act(col("olf", 2 * t), col(sm, SK0), ACT.Copy),
              "at0": lambda: act(view(sm, SA0, SA0 + 16), pickv(view("tab", 0, H), col(of, OK0)), ACT.Copy),
@@ -313,11 +355,22 @@ def build(g, core, T, topo, rank):
              "list0": lambda: copy(view(of, OE0, OE0 + 10), view(sm, SE0, SE0 + 10)),
              "col0": lambda: tt(view("sg", 0, 4), view("pd", 0, 1537, 512), view("zh%d" % (t - 1), 0, 3 * C + 1, C), ALU.add),
              "sign": lambda: ts(col(sm, SC), col("pr", 0), 0.0, 0.5, ALU.is_gt, ALU.subtract),
+             "signs": lambda: act(col(sm, SC), col("pr", 0), ACT.Sign, bias=-TINY),
+             "minus": lambda: act(col(sm, SCS), col("pr", 0), ACT.Sign, scale=-1.0, bias=TINY),
+             "slot": lambda: act(view(dist, 10 * H, 10 * H + 10), view("cnf", 10 * t, 10 * t + 10), ACT.Abs, scale=-1.0, bias=col("tab", H)),
+             "index": lambda: ts(col(of, OH), col(sm, SH), 10.0, col("pm", 0), ALU.mult, ALU.add),
+             "pull": lambda: copy(view(of, OG, OG + 16), pickv(view(dist, 0, 10 * H + 10), col(of, OH))),
              "fore": lambda: act(col(sm, SCS), col(sm, SC), ACT.Copy, scale=-back),
              "back": lambda: act(col(sm, SCN), col(sm, SC), ACT.Copy, scale=back)}
+        for c in range(10):
+            d["row%d" % c] = lambda c=c: act(view(dist, c, 10 * H, 10), view("tab", 0, H), ACT.Abs, scale=-1.0, bias=col("cnf", 10 * t + c))
+        for b in range(2):
+            for a, name in ((0, "ownl"), (H, "ownh")):
+                d["%s%d" % (name, b)] = lambda b=b, a=a: act(view("bh%d" % t, C * b + a, C * b + a + H), plane(b, a, H), ACT.Copy, scale=-back)
         for b in range(4):
             d["unit%d" % b] = lambda b=b: quant("qe", "se", 128 * b, 128 * b + 128, "em", 3 - b)
             d["half%d" % b] = lambda b=b: half(b)
+            d["halfv%d" % b] = lambda b=b: ts(view("zh%d" % t, C * b, C * b + C), plane(b), 32.0 if t == 0 else 0.5, None, ALU.mult)
             d["beam%d" % b] = lambda b=b: beam(b, 0)
             d["high%d" % b] = lambda b=b: beam(b, H)
             d["tail%d" % b] = lambda b=b: tail(b)
@@ -332,14 +385,22 @@ def build(g, core, T, topo, rank):
 
     def do(names, t):
         for name in names.split():
-            S[t + 1][name[:-1]]() if name[-1] == "+" else S[t][name]()
+            if name[-2] == "@":
+                if name[0] != "?" or t == int(name[-1]) - 1:
+                    S[int(name[-1])][name[:-2].lstrip("?")]()
+            else:
+                S[t + name.count("+")][name.rstrip("+")]()
 
     do(ORDER["first"], 0)
     for t in range(R):
         if t:
-            do("landed " + ("loadv " if t == 1 else "qv ") + ORDER["chain"], t)
+            late = ORDER["late"].split() if t == 1 else []
+            do(" ".join(n for n in ["landed"] + ORDER["chain"].split() if n not in late), t)
         if t < R - 1:
-            do(ORDER["window"] + ("" if t else " " + ORDER["spare"]), t)
+            do(ORDER["window%d" % t], t)
+            if t == 0:
+                do(ORDER["late"], 1)
+                do(ORDER["spare"], 0)
         else:
             do(ORDER["last"], t)
 

from concourse.mybir import dt, AluOpType, ActivationFunctionType

C, H, R = 320, 160, 3
STEP = [1, 2, 4]
LOW = -1.0e29
TOP = H * H
TINY = 1.0e-37
SSIGN = True
OWN = True
SEEK = False
CUT = 6
BF, F32, I32, U16, U8, MX = "bfloat16", "float32", "int32", "uint16", "uint8", "float8_e4m3fn_x4"

SCRATCH = {
    "pd": ("psum", [128, 2048], F32), "pr": ("psum", [128, 2048], F32),
    "ut": ("sbuf", [128, 512], BF), "qu": ("sbuf", [128, 128], MX), "su": ("sbuf", [128, 128], U8),
    "qup": ("sbuf", [128, 128], MX), "sup": ("sbuf", [128, 128], U8),
    "uli": ("sbuf", [128, 8], I32), "ul16": ("sbuf", [128, 8], U16),
    "vt": ("sbuf", [128, 512], BF), "qv": ("sbuf", [128, 128], MX), "sv": ("sbuf", [128, 128], U8),
    "wq": ("sbuf", [128, 512], MX), "wp": ("sbuf", [128, 512], U8),
    "ones": ("sbuf", [128, 128], BF), "idn": ("sbuf", [128, 128], BF), "em": ("sbuf", [128, 528], BF),
    "qe": ("sbuf", [128, 512], MX), "se": ("sbuf", [128, 512], U8),
    "bt": ("sbuf", [128, 4 * C], BF),
    "sg": ("sbuf", [128, 512], BF),
    "coi": ("sbuf", [128, 20], I32), "cof": ("sbuf", [128, 20], F32), "co16": ("sbuf", [128, 20], U16),
    "cni": ("sbuf", [128, 30], I32), "cnf": ("sbuf", [128, 30], F32),
    "ramp": ("sbuf", [128, C], F32), "tab": ("sbuf", [128, 336], F32),
    "dm": ("sbuf", [128, TOP + 8], F32),
    "dif": ("sbuf", [128, 176], F32), "past": ("sbuf", [128, 168], F32), "sum": ("sbuf", [128, 168], F32),
    "pi": ("sbuf", [128, 8], I32), "pm": ("sbuf", [128, 8], F32),
    "olb": ("sbuf", [128, 8], F32), "olf": ("sbuf", [128, 8], F32),
    "ysb": ("sbuf", [128, C], F32),
    "junk": ("sbuf", [128, 9 * H], BF),
}
for _t in range(R + 1):
    SCRATCH["xt%d" % _t] = ("sbuf", [128, 4 * C], BF)
    SCRATCH["qx%d" % _t] = ("sbuf", [128, C], MX)
    SCRATCH["sx%d" % _t] = ("sbuf", [128, C], U8)
for _t in range(R):
    if _t > 0:
        SCRATCH["z%d" % _t] = ("sbuf", [128, 4 * C], BF)
        SCRATCH["bh%d" % _t] = ("sbuf", [128, 2 * C], BF)
        SCRATCH["dist%d" % _t] = ("sbuf", [128, 10 * H + 16], F32)
    if _t < R - 1:
        SCRATCH["zh%d" % _t] = ("sbuf", [128, 4 * C], BF)
    SCRATCH["cb%d" % _t] = ("sbuf", [128, 4 * C], BF)
    SCRATCH["e%d" % _t] = ("sbuf", [128, 4 * H], F32)
    SCRATCH["gt%d" % _t] = ("sbuf", [128, 4 * H], BF)
    SCRATCH["gq%d" % _t] = ("sbuf", [128, H], MX)
    SCRATCH["gs%d" % _t] = ("sbuf", [128, H], U8)
    SCRATCH["lq%d" % _t] = ("sbuf", [128, H], MX)
    SCRATCH["ls%d" % _t] = ("sbuf", [128, H], U8)
    SCRATCH["qs%d" % _t] = ("sbuf", [128, 128], MX)
    SCRATCH["ss%d" % _t] = ("sbuf", [128, 128], U8)
    SCRATCH["run%d" % _t] = ("sbuf", [128, 168], F32)
    SCRATCH["sm%d" % _t] = ("sbuf", [128, 96], F32)
    SCRATCH["of%d" % _t] = ("sbuf", [128, 96], U16)

NPOOL = 140
SEMAPHORES = ["sent", "arr0", "arr1", "arr2"] + ["s%d" % _i for _i in range(NPOOL)]

ALU, ACT = AluOpType, ActivationFunctionType
SC, SCS, SCN, SD, SK0, SE1, SH, SE0, SAH, SA0 = 0, 1, 2, 16, 30, 32, 42, 48, 64, 80
OG, OK0, OE1, OH, OE0, OK1, OG4 = 0, 16, 18, 28, 30, 40, 42

LOADS = [("s", "u"), ("y", "x1 x0 co b0 cn bm wc ws v")]
def rows(a, b, t):
    return " ".join("row%d@%d" % (c, t) for c in range(a, b))


START = "back neg1 far0 neg2 neg3 e1_0 e1_1 list0 e1_2 "
WINDOW = START + "half0 e1_3 e0_0 half1 %s q1+ e0_1 e0_2 scan1+ high0+ count1+ e0_3 high1+ %s ownh0+ ownh1+ keep0 %s"
ORDER = {
    "first": "units qu unit0 picku picks q1 q0 co16 scan1 tab0 unit1 scan0 count1 tab1v list1 cnf counth at1 score count0 onlyh "
             "unit2 cof ath signs onlyk farh lists0 lists2 lists1 lists3 fore far1 at0 tail0 tail2 tail1 tail3 negv0 send only1",
    "chain": "list1 q0 at1 slot far1 high2 high3 scan0 beam0 counth count0 col0 beam1 ownl0 score index ownl1 beam2 pull listk "
             "signs minus at0 beam3 tail0 tail2 tail1 tail3 negv0 send",
    "window0": WINDOW % (rows(0, 7, 1), "halfv2 halfv3", rows(7, 10, 1) + " " + rows(0, 6, 2)),
    "window1": WINDOW % (rows(6, 10, 2), "half2 half3", ""),
    "late": "list1 at1 slot far1",
    "spare": "place unit3 pm qv",
    "last": START + "e1_3 e0_0 q1+ e0_1 e0_2 e0_3 keep0 peaks out1",
}


def build(g, core, T, topo, rank):
    ops = []
    Q = {"g": g, "v": g.vector, "s": g.scalar, "t": g.tensor, "y": g.sync}

    def view(name, a, b, step=1):
        m = 0
        for c in range(a, b, step):
            m |= 1 << (c // 512 if name in ("pd", "pr") else c)
        ap = T[name][:, a:b] if step == 1 else T[name][:, a:b:step]
        return (ap, [(name, m)])

    def pickv(win, off):
        return (win[0].indirect(off[0]), win[1] + off[1])

    def op(q, kind, fn, reads, writes):
        rd, wr = [], []
        for x in reads:
            if isinstance(x, tuple):
                rd += x[1]
        for x in writes:
            wr += x[1]
        ops.append({"q": q, "kind": kind, "fn": fn, "rd": rd, "wr": wr, "set": None})

    def bundle(name):
        ops[-1]["set"] = name

    def A(x):
        return x[0] if isinstance(x, tuple) else x

    def dma(q, out, src, after=None):
        op(q, "dma", lambda: Q[q].dma_start(A(out), A(src)), [src, after], [out] if isinstance(out, tuple) else [])

    def bits(x):
        return (x[0].bitcast(dt.uint8), x[1])

    def copy(out, src):
        op("v", "c", lambda: g.vector.tensor_copy(out[0], src[0]), [src], [out])

    def fill(out, val):
        op("v", "c", lambda: g.vector.memset(out[0], val), [], [out])

    def tt(out, a, b, o):
        op("v", "c", lambda: g.vector.tensor_tensor(out[0], a[0], b[0], o), [a, b], [out])

    def ts(out, a, s1, s2, o0, o1=None):
        if o1 is None:
            op("v", "c", lambda: g.vector.tensor_scalar(out[0], a[0], A(s1), None, o0), [a, s1], [out])
        else:
            op("v", "c", lambda: g.vector.tensor_scalar(out[0], a[0], A(s1), A(s2), o0, o1), [a, s1, s2], [out])

    def scan(out, d0, d1, first=LOW, o0=ALU.max, o1=ALU.max):
        op("v", "c", lambda: g.vector.tensor_tensor_scan(out[0], d0[0], d1[0], first, o0, o1), [d0, d1], [out])

    def act(out, src, func, scale=None, bias=None, acc=None):
        kw = {}
        if scale is not None:
            kw["scale"] = A(scale)
        if bias is not None:
            kw["bias"] = A(bias)
        if acc is not None:
            kw["accum_out"] = acc[0]
        op("s", "c", lambda: g.scalar.activation(out[0], src[0], func, **kw), [src, scale, bias],
           [out] + ([acc] if acc is not None else []))

    def quant(q, s, a, b, tile, t0):
        oq, os_, src = view(q, a, b), view(s, a, b), view(tile, t0, t0 + 4 * (b - a))
        op("v", "c", lambda: g.vector.quantize_mx(oq[0], os_[0], src[0]), [src], [oq, os_])

    def mm(ps, bank, lq, ls, la, rq, rs, a, b):
        out = view(ps, 512 * bank, 512 * bank + b - a)
        l0, l1, r0, r1 = view(lq, la, la + 128), view(ls, la, la + 128), view(rq, a, b), view(rs, a, b)
        op("t", "c", lambda: g.tensor.matmul_mx(out[0], l0[0], l1[0], r0[0], r1[0], True, True), [l0, l1, r0, r1], [out])

    def col(name, c, n=1):
        return view(name, c, c + n)

    peers = [T.cores[(rank + s) % len(T.cores)] for s in STEP]
    mask = topo.mask(core, peers[0])
    for p in peers:
        mask &= topo.mask(core, p)
    nen = bin(mask).count("1")

    def send(t):
        rid, pid = topo.addr(peers[t], core)
        arr = T.sem["arr%d" % t]
        cq, cs = view("gq%d" % t, 0, H), view("gs%d" % t, 0, H)
        quant("gq%d" % t, "gs%d" % t, 0, H, "gt%d" % t, 0)
        op("g", "remote", lambda: g.remote_dma(T["lq%d" % t][:, 0:H].bitcast(dt.uint8), cq[0].bitcast(dt.uint8),
                                               arr, T.sem.sent, pid, rid, mask), [cq], [])
        op("g", "remote", lambda: g.remote_dma(T["ls%d" % t][:, 0:H], cs[0], arr, T.sem.sent, pid, rid, mask), [cs], [])

    loads = {"u": lambda q: dma(q, view("ut", 0, 512), T.u[:, 0:512]),
             "x1": lambda q: dma(q, view("xt0", 4 * H, 4 * C), T.x[:, 4 * H:4 * C]),
             "x0": lambda q: dma(q, view("xt0", 0, 4 * H), T.x[:, 0:4 * H]),
             "x": lambda q: dma(q, view("xt0", 0, 4 * C), T.x[:, 0:4 * C]),
             "co": lambda q: dma(q, view("coi", 0, 20), T.co[:, 0:20]),
             "cn": lambda q: dma(q, view("cni", 0, 30), T.cn[:, 0:30]),
             "b0": lambda q: dma(q, view("sg", 0, 8), T.bm[:, 0:8]),
             "bm": lambda q: dma(q, view("bt", 0, 4 * C), T.bm[:, 0:4 * C]),
             "wc": lambda q: dma(q, bits(view("wq", 0, 512)), T.wc[:, 0:2048], after=col("xt0", 0)),
             "ws": lambda q: dma(q, view("wp", 0, 512), T.ws[:, 0:512]),
             "v": lambda q: dma(q, view("vt", 0, 512), T.v[:, 0:512])}
    for q, names in LOADS:
        for name in names.split():
            loads[name](q)

    fill(view("ones", 0, 128), 1.0)
    o_ = view("uli", 0, 8)
    op("g", "c", lambda: g.iota(o_[0], [[16, 8]], 0, 0), [], [o_])
    i_, n_ = view("idn", 0, 128), view("ones", 0, 128)
    op("g", "c", lambda: g.affine_select(i_[0], n_[0], [[-1, 128]], ALU.is_equal, 0.0, 0, 1), [n_], [i_])
    r_ = view("ramp", 0, C)
    op("g", "c", lambda: g.iota(r_[0], [[1, C]], 0, 0, allow_small_or_imprecise_dtypes=True), [], [r_])
    p_ = col("pi", 0)
    op("g", "c", lambda: g.iota(p_[0], [[1, 1]], 0, 1), [], [p_])
    fill(view("dm", 0, TOP, H), LOW)
    fill(view("em", 0, 528), 0.0)
    copy(view("ul16", 0, 8), view("uli", 0, 8))
    fill(view("sg", 8, 512), 0.0)

    njunk = [0]

    def steps(t):
        sm, of, cb, gt, run = "sm%d" % t, "of%d" % t, "cb%d" % t, "gt%d" % t, "run%d" % t
        xo, xn, q, s = "xt%d" % t, "xt%d" % (t + 1), "qx%d" % t, "sx%d" % t
        back = (-1.0 if t == 0 else -1.0 / 64) * (0.5 if SSIGN else 1.0)
        dist = "dist%d" % t
        slot = "dif" if t and SEEK else "tab"

        def count(name, base, top, out):
            j = njunk[0]
            njunk[0] += 1
            act(view("junk", H * j, H * j + H), view(name, base, base + H), ACT.Sign, scale=-1.0, bias=col(name, top), acc=out)

        def plane(b, a=0, n=C):
            if t == 0:
                return view("bt", 4 * a + b, 4 * (a + n), 4)
            return view("z%d" % t, C * b + a, C * b + a + n)

        def q1():
            quant(q, s, H, C, xo, 4 * H)
            if t < R:
                mm("pd", 3, "qup", "sup", 0, q, s, H, C)
            if 0 < t < R:
                for b in range(4):
                    mm("pr", b, "wq", "wp", 128 * b, q, s, H, C)

        def q0():
            quant(q, s, 0, H, xo, 0)
            if t < R:
                mm("pr", 0, "qup", "sup", 0, q, s, 0, H + 2)
            if 0 < t < R:
                for b in range(4):
                    mm("pd", b, "wq", "wp", 128 * b, q, s, 0, H)

        def landed():
            lq, ls = "lq%d" % (t - 1), "ls%d" % (t - 1)
            op(None, "arrive", ("arr%d" % (t - 1), 2 * nen), [], [view(lq, 0, H), view(ls, 0, H)])
            for b in range(4):
                mm("pd", b, "qe", "se", 128 * b, lq, ls, 0, H)
                tt(view(xo, b, 4 * H, 4), view("e%d" % (t - 1), H * b, H * b + H), view("pd", 512 * b, 512 * b + H), ALU.subtract)

        def picku():
            o, i, l = view("qup", 0, 128), view("qu", 0, 128), view("ul16", 0, 8)
            op("v", "c", lambda: g.vector.tensor_copy(o[0].bitcast(dt.uint32), i[0].bitcast(dt.uint32).indirect(l[0])), [i, l], [o])

        def score():
            quant("qs%d" % t, "ss%d" % t, 0, 128, "sg", 0)
            mm("pr", 0, "qup", "sup", 0, "qs%d" % t, "ss%d" % t, 0, 128)

        def beam(b, a):
            tt(view("z%d" % t, C * b + a, C * b + a + H), view("pr" if a else "pd", 512 * b, 512 * b + H),
               view("zh%d" % (t - 1), C * b + a, C * b + a + H), ALU.add)

        def tail(b):
            if t == 0:
                src = pickv(view("bt", 0, 4 * C), view(of, OG4 + 10 * b, OG4 + 10 * b + 10))
            else:
                src = pickv(plane(b), view(of, OG, OG + 10))
            if b < 2 and t and OWN:
                src = pickv(view("bh%d" % t, C * b, C * b + C), view(of, OG, OG + 10))
                act(view(gt, b, 4 * H, 4), src, ACT.Copy, scale=col(sm, SC))
            elif b < 2:
                act(view(gt, b, 4 * H, 4), src, ACT.Copy, scale=col(sm, SCS if t or SSIGN else SC))
            else:
                ts(view(gt, b, 4 * H, 4), src, col(sm, SC), -back, ALU.mult, ALU.mult)

        def part(vec):
            a, n = (CUT, 10) if vec else (0, CUT)
            out, src = view(gt, 64 * a + 1, 64 * n, 4), pickv(plane(1), view(of, OG + a, OG + n))
            if vec:
                ts(out, src, col(sm, SC), -back, ALU.mult, ALU.mult)
            else:
                act(out, src, ACT.Copy, scale=col(sm, SCS))

        def lists(b):
            ts(view(of, OG4 + 10 * b, OG4 + 10 * b + 10), view(sm, SD, SD + 10), 4.0, float(b), ALU.mult, ALU.add)

        def neg(b, vec):
            if vec:
                ts(view(cb, C * b, C * b + C), plane(b), col(sm, SC), back, ALU.mult, ALU.mult)
            elif t and b < 2:
                act(view(cb, C * b, C * b + C), view("bh%d" % t, C * b, C * b + C), ACT.Copy, scale=col(sm, SCS))
            else:
                act(view(cb, C * b, C * b + C), plane(b), ACT.Copy, scale=col(sm, SCN))

        def e1(b):
            tt(view(xn, 4 * H + b, 4 * C, 4), pickv(view(cb, C * b, C * b + C), view(of, OE1, OE1 + 10)),
               view(xo, 4 * H + b, 4 * C, 4), ALU.add)

        def e0(b):
            tt(view("e%d" % t, H * b, H * b + H), pickv(view(cb, C * b, C * b + C), view(of, OE0, OE0 + 10)),
               view(xo, b, 4 * H, 4), ALU.add)

        def half(b):
            act(view("zh%d" % t, C * b, C * b + C), plane(b), ACT.Copy, scale=32.0 if t == 0 else 0.5)

        def out1():
            qn, sn = "qx%d" % R, "sx%d" % R
            dma("y", T.oc[:, 4 * H:4 * C], bits(view(qn, H, C)))
            mm("pr", 0, "qv", "sv", 0, qn, sn, H, C)
            act(view("ysb", H, C), view("pr", 0, H), ACT.Copy)
            dma("y", T.y[:, H:C], view("ysb", H, C))

        def peaks():
            act(view("olf", 1, 6, 2), view("olb", 1, 6, 2), ACT.Identity, bias=float(H))
            dma("y", T.ol[0:8, 0:6], (T.olf[0:128:16, 0:6], view("olf", 0, 6)[1]))

        def count0():
            count(run, 0, H - 1, col(sm, SK0))

        d = {"qu": lambda: quant("qu", "su", 0, 128, "ut", 0), "qv": lambda: quant("qv", "sv", 0, 128, "vt", 0),
             "tail1s": lambda: part(False), "tail1v": lambda: part(True),
             "place": lambda: ts(col("pi", 4), col("pi", 0), 15, None, ALU.bitwise_and),
             "pm": lambda: ts(col("pm", 0), col("pi", 4), 9.0, None, ALU.min),
             "units": lambda: copy(view("em", 3, 515, 4), view("idn", 0, 128)),
             "picku": picku, "picks": lambda: act(view("sup", 0, 128), pickv(view("su", 0, 128), view("ul16", 0, 8)), ACT.Copy),
             "co16": lambda: copy(view("co16", 0, 20), view("coi", 0, 20)),
             "cof": lambda: copy(view("cof", 0, 20), view("coi", 0, 20)),
             "cnf": lambda: copy(view("cnf", 0, 30), view("cni", 0, 30)),
             "tab0": lambda: act(view("tab", 0, H), pickv(view("ramp", 0, C), view("co16", 0, 10)), ACT.Copy),
             "tab1": lambda: act(view("tab", 176, 336), pickv(view("ramp", 0, C), view("co16", 10, 20)), ACT.Copy),
             "q0": q0, "q1": q1, "landed": landed, "score": score, "send": lambda: send(t), "out1": out1, "peaks": peaks,
             "scan1": lambda: scan(view("dm", TOP + 1 - H, TOP + 1), view("pd", 3 * 512, 3 * 512 + H), view("dm", 0, TOP, H)),
             "count1": lambda: count("dm", TOP + 1 - H, TOP, col("olb", 2 * t + 1)),
             "list1": lambda: copy(col(of, OK1), col("olb", 2 * t + 1)),
             "at1": lambda: act(view(slot, H, H + 16), pickv(view("tab", 176, 336), col(of, OK1)), ACT.Copy),
             "far1": lambda: act(view(sm, SE1 - 1, SE1 + 10), view("cof", 9, 20), ACT.Abs, scale=-1.0, bias=col(slot, H)),
             "listk": lambda: copy(view(of, OK0, OE1 + 10), view(sm, SK0, SE1 + 10)),
             "dif": lambda: tt(view("dif", 0, H - 1), view("tab", 0, H - 1), view("tab", 1, H), ALU.subtract),
             "edge": lambda: act(col("dif", H - 1), col("dif", H), ACT.Identity, scale=-1.0, bias=col("tab", H - 1)),
             "found": lambda: ts(view("past", 1, H + 1), view(run, 0, H), col(run, H), None, ALU.is_ge),
             "seek": lambda: scan(view("sum", 0, H + 1), view("past", 0, H + 1), view("dif", 0, H + 1), 0.0, ALU.mult, ALU.add),
             "none": lambda: fill(col("past", 0), 0.0),
             "scan0": lambda: scan(view(run, 0, H + 1), view("pr", 0, H + 1), view("dm", 0, TOP + 1, H)),
             "counth": lambda: count(run, 0, H, col(sm, SH)),
             "listh": lambda: copy(view(of, OE1, OH + 1), view(sm, SE1, SH + 1)),
             "onlyh": lambda: copy(col(of, OH), col(sm, SH)),
             "only1": lambda: copy(view(of, OE1, OE1 + 10), view(sm, SE1, SE1 + 10)),
             "onlyg": lambda: copy(view(of, OG, OG + 10), view(sm, SD, SD + 10)),
             "onlyk": lambda: copy(col(of, OK0), col(sm, SK0)),
             "tab1v": lambda: copy(view("tab", 176, 336), pickv(view("ramp", 0, C), view("co16", 10, 20))),
             "ath": lambda: act(view(sm, SAH, SAH + 16), pickv(view("tab", 0, H + 1), col(of, OH)), ACT.Copy),
             "farh": lambda: act(view(sm, SD, SD + 10), view("cnf", 10 * t, 10 * t + 10), ACT.Abs, scale=-1.0,
                                 bias=col("sum", H) if t and SEEK else col(sm, SAH)),
             "count0": count0,
             "keep0": lambda: act(col("olf", 2 * t), col(sm, SK0), ACT.Copy),
             "at0": lambda: act(view(sm, SA0, SA0 + 16), pickv(view("tab", 0, H), col(of, OK0)), ACT.Copy),
             "far0": lambda: act(view(sm, SE0, SE0 + 10), view("cof", 0, 10), ACT.Abs, scale=-1.0, bias=col(sm, SA0)),
             "list0": lambda: copy(view(of, OE0, OE0 + 10), view(sm, SE0, SE0 + 10)),
             "col0": lambda: tt(view("sg", 0, 4), view("pd", 0, 1537, 512), view("zh%d" % (t - 1), 0, 3 * C + 1, C), ALU.add),
             "sign": lambda: ts(col(sm, SC), col("pr", 0), 0.0, 0.5, ALU.is_gt, ALU.subtract),
             "signs": lambda: act(col(sm, SC), col("pr", 0), ACT.Sign, bias=-TINY),
             "minus": lambda: act(col(sm, SCS), col("pr", 0), ACT.Sign, scale=-1.0, bias=TINY),
             "slot": lambda: act(view(dist, 10 * H, 10 * H + 10), view("cnf", 10 * t, 10 * t + 10), ACT.Abs, scale=-1.0, bias=col("tab", H)),
             "index": lambda: ts(col(of, OH), col(sm, SH), 10.0, col("pm", 0), ALU.mult, ALU.add),
             "pull": lambda: copy(view(of, OG, OG + 16), pickv(view(dist, 0, 10 * H + 10), col(of, OH))),
             "fore": lambda: act(col(sm, SCS), col(sm, SC), ACT.Copy, scale=-back),
             "back": lambda: act(col(sm, SCN), col(sm, SC), ACT.Copy, scale=back)}
        for c in range(10):
            d["row%d" % c] = lambda c=c: act(view(dist, c, 10 * H, 10), view("tab", 0, H), ACT.Abs, scale=-1.0, bias=col("cnf", 10 * t + c))
        for b in range(2):
            for a, name in ((0, "ownl"), (H, "ownh")):
                d["%s%d" % (name, b)] = lambda b=b, a=a: act(view("bh%d" % t, C * b + a, C * b + a + H), plane(b, a, H), ACT.Copy, scale=-back)
        for b in range(4):
            d["unit%d" % b] = lambda b=b: quant("qe", "se", 128 * b, 128 * b + 128, "em", 3 - b)
            d["half%d" % b] = lambda b=b: half(b)
            d["halfv%d" % b] = lambda b=b: ts(view("zh%d" % t, C * b, C * b + C), plane(b), 32.0 if t == 0 else 0.5, None, ALU.mult)
            d["beam%d" % b] = lambda b=b: beam(b, 0)
            d["high%d" % b] = lambda b=b: beam(b, H)
            d["tail%d" % b] = lambda b=b: tail(b)
            d["lists%d" % b] = lambda b=b: lists(b)
            d["neg%d" % b] = lambda b=b: neg(b, False)
            d["negv%d" % b] = lambda b=b: neg(b, True)
            d["e1_%d" % b] = lambda b=b: e1(b)
            d["e0_%d" % b] = lambda b=b: e0(b)
        return d

    S = [steps(t) for t in range(R + 1)]

    def do(names, t):
        for name in names.split():
            if name[-2] == "@":
                if name[0] != "?" or t == int(name[-1]) - 1:
                    S[int(name[-1])][name[:-2].lstrip("?")]()
            else:
                S[t + name.count("+")][name.rstrip("+")]()

    do(ORDER["first"], 0)
    for t in range(R):
        if t:
            late = ORDER["late"].split() if t == 1 else []
            do(" ".join(n for n in ["landed"] + ORDER["chain"].split() if n not in late), t)
        if t < R - 1:
            do(ORDER["window%d" % t], t)
            if t == 0:
                do(ORDER["late"], 1)
                do(ORDER["spare"], 0)
        else:
            do(ORDER["last"], t)

    do("landed q0", R)
    q, s = "qx%d" % R, "sx%d" % R
    mm("pr", 1, "qv", "sv", 0, q, s, 0, H)
    dma("y", T.oc[:, 0:4 * H], bits(view(q, 0, H)))
    copy(view("ysb", 0, H), view("pr", 512, 512 + H))
    for k in range(4):
        dma("y" if k < 2 else "s", T.osc[4 * k:4 * k + 4, 0:C], (T[s][32 * k:32 * k + 4, 0:C], view(s, 0, C)[1]))
    dma("s", T.y[:, 0:H], view("ysb", 0, H))
    return ops, Q, 2 * R * nen


def clash(a, b):
    for n1, m1 in a:
        for n2, m2 in b:
            if n1 == n2 and m1 & m2:
                return True
    return False


def order(ops):
    known, seen, waits = {}, [], []
    for i, o in enumerate(ops):
        ps_i = [x for x in o["rd"] if x[0] in ("pd", "pr")]
        have = known.get(o["q"], 0) if o["q"] else 0
        need = []
        for j in range(i):
            p = ops[j]
            if have >> j & 1 or p["kind"] == "remote" or o["kind"] == "arrive":
                continue
            if clash(o["rd"], p["wr"]) or clash(o["wr"], p["wr"]) or clash(o["wr"], p["rd"]) or (
                    p["q"] != o["q"] and clash(ps_i, p["rd"])):
                need.append(j)
        sets = [ops[j]["set"] for j in need if ops[j]["set"]]
        need += [j for j in range(i) if ops[j]["set"] in sets and j not in need and not have >> j & 1]
        implied = 0
        for j in need:
            implied |= seen[j]
        need = [j for j in need if not implied >> j & 1]
        for j in need:
            have |= seen[j] | 1 << j
        if o["q"]:
            known[o["q"]] = have
        seen.append(have)
        waits.append(need)
    return waits, seen


def rank_program(g, core, T, topo):
    rank = T.rank_of(core)
    if rank is None:
        return
    ops, Q, sent = build(g, core, T, topo, rank)
    waits, seen = order(ops)
    n = len(ops)
    tails = {}
    for j, o in enumerate(ops):
        if o["kind"] == "dma" and not o["wr"]:
            tails.setdefault(o["q"], []).append(j)
    ends = sorted(tails)
    for q in ends:
        waits.append(tails[q])
    waiters = {}
    for i, w in enumerate(waits):
        for j in w:
            waiters.setdefault(j, []).append(i)

    def queue(i):
        return ops[i]["q"] if i < n else ends[i - n]

    rides = {}
    for j in sorted(waiters, reverse=True):
        if ops[j]["kind"] != "c":
            continue
        for k in range(j + 1, waiters[j][0]):
            if k in waiters and k not in rides and ops[k]["kind"] == "c" and ops[k]["q"] == ops[j]["q"] and all(
                    any(queue(m) == queue(i) and m <= i for m in waiters[k]) for i in waiters[j]):
                rides[j] = k
                break
    for j in rides:
        for i in waiters[j]:
            waits[i].remove(j)
    groups, home = {}, {}
    for j in sorted(waiters):
        if ops[j]["kind"] != "arrive" and j not in rides:
            home[j] = (ops[j]["kind"], tuple(waiters[j]))
            groups.setdefault(home[j], []).append(j)
    for j in sorted(rides):
        groups[home[rides[j]]].append(j)
    token, pool = {}, []
    for key in sorted(groups, key=lambda k: min(groups[k])):
        mem = groups[key]
        inc = 16 if key[0] == "dma" else 1
        slot = None
        if len(pool) < NPOOL:
            slot = {"name": "s%d" % len(pool), "kind": key[0], "count": 0, "last": []}
            pool.append(slot)
        else:
            for sl in pool:
                if sl["kind"] == key[0] and all(seen[m] >> j & 1 for m in mem for j in sl["last"]):
                    slot = sl
                    break
        slot["count"] += inc * len(mem)
        slot["last"] = mem
        for j in mem:
            token[j] = (slot["name"], slot["count"], inc)
    for j, o in enumerate(ops):
        if o["kind"] == "arrive":
            token[j] = (o["fn"][0], o["fn"][1], 0)

    def wait(q, js):
        done = []
        for j in js:
            tk = token[j][:2]
            if tk not in done:
                done.append(tk)
                Q[q].wait_ge(T.sem[tk[0]], tk[1])

    for i, o in enumerate(ops):
        if o["kind"] == "arrive":
            continue
        wait(o["q"], waits[i])
        ins = o["fn"]()
        if i in token:
            ins.then_inc(T.sem[token[i][0]], token[i][2])
    for k, q in enumerate(ends):
        wait(q, waits[n + k])
    g.wait_ge(T.sem.sent, sent)
